import numpy as np
import ml_dtypes


def mxq(x, axis, fmt="e4m3"):
    dtype, down = {"e4m3": (ml_dtypes.float8_e4m3fn, 7), "e5m2": (ml_dtypes.float8_e5m2, 14)}[fmt]
    v = np.moveaxis(np.asarray(x, np.float32).astype(ml_dtypes.bfloat16).astype(np.float64), axis, -1)
    blocks = v.reshape(v.shape[:-1] + (-1, 32))
    amax = np.abs(blocks).max(-1, keepdims=True)
    byte = np.maximum(np.where(amax > 0, np.frexp(amax)[1] - 1 + 127, 0) - down, 1)
    scale = np.exp2(byte - 127.0)
    codes = (blocks / scale).astype(np.float32).astype(dtype).astype(np.float64)
    return np.moveaxis((codes * scale).reshape(v.shape), -1, axis)


WIDE = False


def mx_kscale(k):
    if not WIDE:
        return np.ones(k)
    levels = np.array([10, -10, 5, -5, 0])
    if k % 512:
        return np.exp2(np.random.permutation(np.resize(levels, k // 32))).repeat(32)
    a = np.empty((k // 512, 16))
    for p in range(k // 512):
        a[p, :8] = np.random.permutation(np.resize(levels, 8))
        for g in range(8):
            far = levels[np.abs(levels - a[p, g]) >= 10]
            a[p, g + 8] = far[np.random.randint(len(far))]
    return np.exp2(a.ravel()).repeat(32)


BF16 = ml_dtypes.bfloat16


def bf(x):
    return np.asarray(x, np.float32).astype(BF16)


def f64(x):
    return np.asarray(x).astype(np.float64)


M, N, K, T, R, H = 512, 1024, 512, 512, 4, 1024

X_STD = 0.5
ATTR_STD = 0.16
ID_STD = 0.12
PAIR_GAIN = 0.1


def setup_inputs():
    s, t, v = mx_kscale(K), mx_kscale(N), mx_kscale(H)
    D = T * R
    return {"x": bf(np.random.standard_normal((M, N)) * X_STD * t),
            "attr": bf(np.random.standard_normal((N, K)) * s / t[:, None]),
            "w_attr": bf(np.random.standard_normal((K, D)) * ATTR_STD / np.sqrt(K) / s[:, None]),
            "ids": bf(np.random.standard_normal((N, D)) * ID_STD / t[:, None]),
            "pair": bf(PAIR_GAIN * (1.0 + 0.1 * np.random.standard_normal(D))),
            "lin": bf(np.random.standard_normal((N, T)) * 0.7 / X_STD / np.sqrt(N) / t[:, None]),
            "b0": bf(np.random.standard_normal(T) * 0.3),
            "u": bf(np.random.standard_normal((N, H)) / X_STD / np.sqrt(N) / t[:, None] * v),
            "b1": bf(np.random.standard_normal(H) * 0.3 * v),
            "w2": bf(np.random.standard_normal((H, T)) * 1.4 / np.sqrt(H) / v[:, None])}


def reference(x, attr, w_attr, ids, pair, lin, b0, u, b1, w2):
    x = f64(x)
    e = (mxq(f64(attr), 1, "e4m3") @ mxq(f64(w_attr), 0, "e4m3")) + f64(ids)
    xq = mxq(x, 1, "e4m3")
    total = xq @ mxq(e, 0, "e4m3")
    squares = mxq(x * x, 1, "e4m3") @ mxq(e * e, 0, "e4m3")
    inter = f64(pair) * (total * total - squares)
    fm = 0.5 * inter.reshape(M, R, T).sum(axis=1)
    first = (xq @ mxq(f64(lin), 0, "e4m3")) + f64(b0)
    hidden = np.maximum((xq @ mxq(f64(u), 0, "e4m3")) + f64(b1), 0.0)
    deep = mxq(hidden, 1, "e4m3") @ mxq(f64(w2), 0, "e4m3")
    return first + fm + deep

@@ -1,0 +1,433 @@
+from contextlib import ExitStack
+
+import concourse.mybir as mybir
+from concourse.masks import make_identity
+
+M, N, K, T, R, H = 512, 1024, 512, 512, 4, 1024
+D = T * R
+FLOPS = 2 * (N * K * D + 2 * M * N * D + M * N * T + M * N * H + M * H * T)
+
+F32 = mybir.dt.float32
+BF16 = mybir.dt.bfloat16
+U32 = mybir.dt.uint32
+U8 = mybir.dt.uint8
+FP8X4 = mybir.dt.float8_e4m3fn_x4
+ACT = mybir.ActivationFunctionType
+ALU = mybir.AluOpType
+
+P = 128
+PASS = 512
+UNITS = [(0, j) for j in range(4)] + [(1, j) for j in range(4)] + [(r, j) for j in range(4) for r in (2, 3)]
+
+
+def tile_attribute_fm_plus_mlp_f4_kernel(tc, x, attr, w_attr, ids, pair, lin, b0, u, b1, w2, out):
+    nc = tc.nc
+    with ExitStack() as ctx:
+        sb = ctx.enter_context(tc.tile_pool(name="sb", bufs=1))
+        ps = ctx.enter_context(tc.psum_pool(name="ps", bufs=1))
+        ctx.enter_context(tc.manual_schedule())
+
+        def tiles(name, count, shape, dtype):
+            return [sb.tile(shape, dtype, name="%s%d" % (name, i), align_bytes=64) for i in range(count)]
+
+        def mx_tiles(name, count, width):
+            return list(zip(tiles(name + "_c", count, [P, width], U32), tiles(name + "_s", count, [P, width], U8)))
+
+        banks = [ps.tile([P, 512], F32, name="bank%d" % i) for i in range(8)]
+        e_banks, t_bank, q_bank, aux = banks[0:2], banks[2], banks[3], banks[4:8]
+
+        attr_raw = tiles("attr_raw", 2, [P, 2048], BF16)
+        x_raw = tiles("x_raw", 2, [P, 2048], BF16)
+        w_first = tiles("w_first", 2, [P, 1024], BF16)
+        ids_first = tiles("ids_first", 4, [P, 1024], BF16)
+        w_raw = tiles("w_raw", 3, [P, 2048], BF16)
+        ids_raw = tiles("ids_raw", 6, [P, 2048], BF16)
+        u_raw = tiles("u_raw", 4, [P, 2048], BF16)
+        lw_raw = tiles("lw_raw", 2, [P, 4096], BF16)
+        vec_raw = tiles("vec_raw", 1, [P, P], BF16)[0]
+        vec_rows = tiles("vec_rows", 1, [P, P], F32)[0]
+        vec = tiles("vec", 1, [P, 20], F32)[0]
+        b1_raw = tiles("b1_raw", 1, [P, 8], BF16)[0]
+        ident = tiles("ident", 1, [P, P], F32)[0]
+        warm = tiles("warm", 2, [P, 1], F32)
+
+        stage = tiles("stage", 7, [P, 2048], BF16)
+        attr_q = mx_tiles("attr", 2, 512)
+        x_q = mx_tiles("x", 2, 512)
+        xx_q = mx_tiles("xx", 2, 512)
+        w_q = mx_tiles("w", 8, 256)
+        u_q = mx_tiles("u", 4, 512)
+        h_q = mx_tiles("h", 2, 512)
+        lw_q = mx_tiles("lw", 4, 512)
+        e_q = mx_tiles("e", 2, 256)
+        ee_q = mx_tiles("ee", 2, 256)
+        e32 = tiles("e32", 2, [P, 1024], F32)
+        e_bf = tiles("e_bf", 1, [P, 1024], BF16)[0]
+        ee_bf = tiles("ee_bf", 2, [P, 1024], BF16)
+        h_bf = tiles("h_bf", 2, [P, 2048], BF16)
+        tt = tiles("tt", 2, [P, 512], F32)
+        y = tiles("y", 12, [P, 512], F32)
+        res = tiles("res", 2, [P, 512], F32)
+        used = {"stage": 0, "aux": 0}
+
+        def take(ring, name):
+            used[name] = used[name] + 1
+            return ring[(used[name] - 1) % len(ring)]
+
+        def copy(eng, dst, src):
+            if eng == "S":
+                nc.scalar.copy(out=dst, in_=src)
+            elif eng == "V":
+                nc.vector.tensor_copy(out=dst, in_=src)
+            else:
+                nc.gpsimd.tensor_scalar(out=dst, in0=src, scalar1=1.0, scalar2=0.0, op0=ALU.mult, op1=ALU.add)
+
+        def quantize(q, src):
+            nc.vector.quantize_mx(out=q[0][:].bitcast(FP8X4), scales=q[1][:], in_=src)
+
+        def mx(dst, lhs, lcol, rhs, rcol, n, start, stop):
+            nc.tensor.matmul_mx(
+                out=dst,
+                lhsT=lhs[0][:, lcol : lcol + P].bitcast(FP8X4),
+                lhsT_scale=lhs[1][:, lcol : lcol + P],
+                rhs=rhs[0][:, rcol : rcol + n].bitcast(FP8X4),
+                rhs_scale=rhs[1][:, rcol : rcol + n],
+                start=start,
+                stop=stop,
+            )
+
+        def load_k_first(dst, src):
+            nc.sync.dma_start(out=dst[:].rearrange("p (j c) -> p j c", j=4), in_=src.rearrange("(p j) c -> p j c", j=4))
+
+        def half(i):
+            return slice(PASS * i, PASS * (i + 1))
+
+        def load_ids(r):
+            for g in range(2):
+                load_k_first(ids_raw[2 * (r - 1) + g], ids[half(g), half(r)])
+
+        def load_first_ids(h):
+            for g in range(2):
+                load_k_first(ids_first[2 * h + g], ids[half(g), 256 * h : 256 * (h + 1)])
+
+        def rows4(tile):
+            return tile[:].rearrange("p (j c) -> p j c", j=4)
+
+        def w_view(h):
+            if h < 2:
+                return rows4(w_first[h])
+            return rows4(w_raw[h // 2 - 1])[:, :, 256 * (h % 2) : 256 * (h % 2 + 1)]
+
+        def ids_view(r, jt, g):
+            if r == 0:
+                return rows4(ids_first[2 * (jt // 2) + g])[:, :, P * (jt % 2) : P * (jt % 2 + 1)]
+            return rows4(ids_raw[2 * (r - 1) + g])[:, :, P * jt : P * (jt + 1)]
+
+        def load_x(g):
+            nc.sync.dma_start(out=x_raw[g][:].rearrange("p (s c) -> p s c", s=4), in_=x[:, half(g)].rearrange("(s p) c -> p s c", p=P))
+
+        def load_u(gh):
+            for g in range(2):
+                load_k_first(u_raw[2 * gh + g], u[half(g), half(gh)])
+
+        load_k_first(attr_raw[0], attr[half(0), :])
+        load_k_first(w_first[0], w_attr[:, 0:256])
+        load_k_first(attr_raw[1], attr[half(1), :])
+        load_first_ids(0)
+        load_k_first(w_first[1], w_attr[:, 256:512])
+        load_x(0)
+        load_x(1)
+        load_first_ids(1)
+        load_u(0)
+        nc.sync.dma_start(out=vec_raw[0:16, :], in_=pair.rearrange("(i c) -> i c", c=P))
+        nc.sync.dma_start(out=vec_raw[16:20, :], in_=b0.rearrange("(i c) -> i c", c=P))
+        nc.sync.dma_start(out=b1_raw[:].rearrange("p (g t) -> p g t", g=2), in_=b1.rearrange("(g p t) -> p g t", g=2, t=4))
+        load_k_first(w_raw[0], w_attr[:, half(1)])
+        load_ids(1)
+        load_u(1)
+        load_k_first(w_raw[1], w_attr[:, half(2)])
+        load_k_first(w_raw[2], w_attr[:, half(3)])
+        load_ids(2)
+        load_ids(3)
+        for i, src in enumerate((lin, w2)):
+            nc.sync.dma_start(out=lw_raw[i][:].rearrange("p (g c) -> p g c", g=2), in_=src.rearrange("(g p j) c -> p g (j c)", g=2, j=4))
+
+        make_identity(nc, ident[:])
+        nc.gpsimd.memset(vec_rows[:], 0.0)
+        nc.vector.memset(warm[0][:], 0.0)
+        nc.scalar.activation(out=warm[1][:], in_=warm[0][:], func=ACT.Square)
+
+        def turn(raw, engs):
+            words = raw[:].bitcast(F32)
+            dst = take(stage, "stage")
+            dwords = dst[:].bitcast(F32)
+            for b in range(2):
+                bank = take(aux, "aux")
+                for s in range(2):
+                    for w in range(2):
+                        first = 256 * (2 * b + s)
+                        nc.tensor.transpose(bank[:, P * (2 * s + w) : P * (2 * s + w + 1)], words[:, first + w : first + 256 : 2], ident[:])
+                copy(
+                    engs[b],
+                    dwords[:, 512 * b : 512 * (b + 1)].rearrange("p (s m w) -> p s m w", s=2, w=2),
+                    bank[:].rearrange("p (s w m) -> p s m w", s=2, w=2),
+                )
+            return dst
+
+        def weave(eng, dst, src):
+            copy(eng, dst.rearrange("p (c i j) -> p c j i", i=4, j=4), src.rearrange("p j (c i) -> p c j i", i=4))
+
+        held = {}
+
+        def w_weave(h, eng):
+            dst = take(stage, "stage")
+            weave(eng, dst[:, 0:1024], w_view(h))
+            held["w", h] = dst
+
+        def w_quant(h):
+            quantize(w_q[h], held["w", h][:, 0:1024])
+
+        def u_weave(i, part, eng):
+            if part == 0:
+                held["u", i] = take(stage, "stage")
+            ms = slice(64 * part, 64 * (part + 1))
+            copy(eng, held["u", i][:].rearrange("p (t m j) -> p m j t", t=4, j=4)[:, ms], u_raw[i][:].rearrange("p (j m t) -> p m j t", j=4, t=4)[:, ms])
+
+        def u_quant(i):
+            quantize(u_q[i], held["u", i][:])
+
+        def lw_weave(jt, which, eng):
+            if which == 0:
+                held["lw", jt] = take(stage, "stage")
+            dst = held["lw", jt][:, 1024 * which : 1024 * (which + 1)]
+            src = lw_raw[which][:].rearrange("p (g j c) -> p g j c", g=2, j=4)[:, :, :, P * jt : P * (jt + 1)]
+            copy(eng, dst.rearrange("p (g c i j) -> p g c j i", g=2, i=4, j=4), src.rearrange("p g j (c i) -> p g c j i", i=4))
+
+        def lw_quant(jt):
+            quantize(lw_q[jt], held["lw", jt][:])
+
+        def hidden_mm(i):
+            gh, t = divmod(i, 4)
+            bank = take(aux, "aux")
+            for g in range(2):
+                mx(bank[:], u_q[2 * gh + g], P * t, x_q[g], 0, 512, g == 0, g == 1)
+            held["hb", i] = bank
+
+        def relu(i, eng):
+            gh, t = divmod(i, 4)
+            bank = held["hb", i]
+            dst = h_bf[gh][:, 512 * t : 512 * (t + 1)]
+            if eng == "S":
+                nc.scalar.activation(out=dst, in_=bank[:], func=ACT.Relu, bias=b1_raw[:, i : i + 1])
+            else:
+                nc.vector.tensor_scalar(out=dst, in0=bank[:], scalar1=b1_raw[:, i : i + 1], scalar2=0.0, op0=ALU.add, op1=ALU.max)
+
+        def h_weave(gh, part, eng):
+            if part == 0:
+                held["h", gh] = take(stage, "stage")
+            src = h_bf[gh][:].rearrange("p (j c) -> p j c", j=4)
+            weave(eng, held["h", gh][:, 1024 * part : 1024 * (part + 1)], src[:, :, 256 * part : 256 * (part + 1)])
+
+        def h_quant(gh):
+            quantize(h_q[gh], held["h", gh][:])
+
+        def xx_make(g, eng):
+            dst = take(stage, "stage")
+            if eng == "S":
+                nc.scalar.activation(out=dst[:], in_=held["x", g][:], func=ACT.Square)
+            else:
+                nc.vector.tensor_tensor(out=dst[:], in0=held["x", g][:], in1=held["x", g][:], op=ALU.mult)
+            held["xx", g] = dst
+
+        def vectors():
+            nc.scalar.copy(out=vec_rows[0:20, :], in_=vec_raw[0:20, :])
+            bank = take(aux, "aux")
+            nc.tensor.transpose(bank[:, 0:P], vec_rows[:], ident[:])
+            held["vec"] = bank
+
+        def vectors_out():
+            nc.scalar.activation(out=vec[:, 0:16], in_=held["vec"][:, 0:16], func=ACT.Copy, scale=0.5)
+            nc.scalar.copy(out=vec[:, 16:20], in_=held["vec"][:, 16:20])
+
+        def y_of(n):
+            return y[n] if n < 8 else y[8 + n % 4]
+
+        def embed(n, gs=(0, 1)):
+            r, jt = UNITS[n]
+            for g in gs:
+                for t in range(4):
+                    mx(e_banks[g][:, P * t : P * (t + 1)], attr_q[g], P * t, w_q[2 * r + jt // 2], P * (jt % 2), P, True, True)
+
+        def add_ids(n, gs=(0, 1)):
+            r, jt = UNITS[n]
+            for g in gs:
+                nc.vector.tensor_tensor(
+                    out=e32[n % 2][:].rearrange("p (t g c) -> p t g c", t=4, g=2)[:, :, g, :],
+                    in0=e_banks[g][:].rearrange("p (t c) -> p t c", t=4),
+                    in1=ids_view(r, jt, g),
+                    op=ALU.add,
+                )
+
+        def e_round(n, eng):
+            copy(eng, e_bf[:].rearrange("p (c t) -> p c t", t=4), e32[n % 2][:].rearrange("p (t c) -> p c t", t=4))
+
+        def e_square(n):
+            nc.scalar.activation(
+                out=ee_bf[n % 2][:].rearrange("p (c i t) -> p c t i", i=4, t=4),
+                in_=e32[n % 2][:].rearrange("p (t c i) -> p c t i", i=4, t=4),
+                func=ACT.Square,
+            )
+
+        def e_quant(n):
+            quantize(e_q[n % 2], e_bf[:])
+            quantize(ee_q[n % 2], ee_bf[n % 2][:])
+
+        def products(n):
+            for g in range(2):
+                mx(t_bank[:], e_q[n % 2], P * g, x_q[g], 0, 512, g == 0, g == 1)
+            for g in range(2):
+                mx(q_bank[:], ee_q[n % 2], P * g, xx_q[g], 0, 512, g == 0, g == 1)
+
+        def total_square(n):
+            nc.scalar.activation(out=tt[n % 2][:], in_=t_bank[:], func=ACT.Square)
+
+        def subtract(n):
+            nc.vector.tensor_tensor(out=y_of(n)[:], in0=tt[n % 2][:], in1=q_bank[:], op=ALU.subtract)
+
+        def f_bank(jt):
+            return e_banks[0] if jt == 3 else aux[0]
+
+        def linear_and_deep(jt):
+            bank = f_bank(jt)
+            for i, rhs in enumerate(x_q + h_q):
+                mx(bank[:], lw_q[jt], P * i, rhs, 0, 512, i == 0, i == 3)
+
+        def scale(n, eng):
+            r, jt = UNITS[n]
+            gain = vec[:, 4 * r + jt : 4 * r + jt + 1]
+            if r == 3:
+                nc.vector.scalar_tensor_tensor(out=y_of(n)[:], in0=y_of(n)[:], scalar=gain, in1=f_bank(jt)[:], op0=ALU.mult, op1=ALU.add)
+            else:
+                shift = vec[:, 16 + jt : 17 + jt] if r == 2 else 0.0
+                engine = nc.vector if eng == "V" else nc.gpsimd
+                engine.tensor_scalar(out=y_of(n)[:], in0=y_of(n)[:], scalar1=gain, scalar2=shift, op0=ALU.mult, op1=ALU.add)
+
+        def gather(jt, rs):
+            bank = aux[1 + jt % 3]
+            for r in rs:
+                src = y_of(UNITS.index((r, jt)))
+                for s in range(4):
+                    nc.tensor.matmul(
+                        out=bank[:, P * s : P * (s + 1)],
+                        lhsT=src[:, P * s : P * (s + 1)],
+                        rhs=ident[:],
+                        start=(r == 0 and s == 0),
+                        stop=(r == 3 and s == 3),
+                        is_transpose=True,
+                    )
+
+        def finish(jt, eng):
+            copy(eng, res[jt % 2][:], aux[1 + jt % 3][:])
+            nc.sync.dma_start(
+                out=out[:, P * jt : P * (jt + 1)].rearrange("(s p) c -> p s c", p=P),
+                in_=res[jt % 2][:].rearrange("p (s c) -> p s c", s=4),
+            )
+
+        a0 = turn(attr_raw[0], "SV")
+        w_weave(0, "V")
+        quantize(attr_q[0], a0[:])
+        a1 = turn(attr_raw[1], "SV")
+        w_quant(0)
+        embed(0, (0,))
+        quantize(attr_q[1], a1[:])
+        add_ids(0, (0,))
+        embed(0, (1,))
+        embed(1, (0,))
+        w_weave(1, "S")
+        held["x", 0] = turn(x_raw[0], "SS")
+        add_ids(0, (1,))
+        embed(1, (1,))
+        early = {s: [] for s in range(20)}
+        late = {s: [] for s in range(20)}
+        def x1_turn():
+            held["x", 1] = turn(x_raw[1], "SS")
+        early[1].extend([lambda: w_quant(1), lambda: x1_turn()])
+        late[1].extend([lambda: quantize(x_q[0], held["x", 0][:]), lambda: xx_make(0, "V"), lambda: quantize(x_q[1], held["x", 1][:]), lambda: xx_make(1, "S"), lambda: quantize(xx_q[0], held["xx", 0][:])])
+        early[2].extend([lambda: u_weave(0, 0, "V"), lambda: u_weave(0, 1, "V"), lambda: quantize(xx_q[1], held["xx", 1][:])])
+        late[2].extend([lambda: u_weave(1, 0, "S"), lambda: u_weave(1, 1, "S"), lambda: vectors(), lambda: w_weave(2, "V")])
+        early[3].extend([lambda: vectors_out(), lambda: u_quant(0), lambda: u_quant(1), lambda: hidden_mm(0), lambda: w_quant(2)])
+        late[3].extend([lambda: relu(0, "V"), lambda: w_weave(3, "S"), lambda: u_weave(2, 0, "S")])
+        early[4].extend([lambda: hidden_mm(1)])
+        late[4].extend([lambda: relu(1, "V"), lambda: u_weave(2, 1, "S")])
+        early[5].extend([lambda: hidden_mm(2), lambda: w_quant(3)])
+        late[5].extend([lambda: relu(2, "V"), lambda: u_weave(3, 0, "S"), lambda: u_weave(3, 1, "S")])
+        early[6].extend([lambda: hidden_mm(3), lambda: u_quant(2)])
+        late[6].extend([lambda: relu(3, "V"), lambda: w_weave(4, "S")])
+        early[7].extend([lambda: u_quant(3), lambda: hidden_mm(4), lambda: w_quant(4)])
+        late[7].extend([lambda: relu(4, "V"), lambda: w_weave(6, "S"), lambda: h_weave(0, 0, "S")])
+        early[8].extend([lambda: hidden_mm(5), lambda: w_quant(6)])
+        late[8].extend([lambda: relu(5, "V"), lambda: h_weave(0, 1, "S")])
+        early[9].extend([lambda: hidden_mm(6)])
+        late[9].extend([lambda: relu(6, "V"), lambda: w_weave(5, "S"), lambda: lw_weave(0, 0, "S")])
+        early[10].extend([lambda: hidden_mm(7), lambda: h_quant(0)])
+        late[10].extend([lambda: relu(7, "V"), lambda: lw_weave(0, 1, "S"), lambda: w_weave(7, "S")])
+        early[11].extend([lambda: w_quant(5), lambda: lw_quant(0)])
+        late[11].extend([lambda: h_weave(1, 0, "S"), lambda: h_weave(1, 1, "S"), lambda: gather(0, (0, 1))])
+        early[12].extend([lambda: w_quant(7), lambda: h_quant(1)])
+        late[12].extend([lambda: linear_and_deep(0), lambda: lw_weave(1, 0, "S"), lambda: lw_weave(1, 1, "S"), lambda: gather(0, (2,)), lambda: gather(1, (0, 1))])
+        early[13].extend([])
+        late[13].extend([lambda: lw_weave(2, 0, "S"), lambda: lw_weave(2, 1, "S"), lambda: gather(0, (3,)), lambda: gather(2, (0, 1))])
+        early[14].extend([lambda: lw_quant(1), lambda: linear_and_deep(1)])
+        late[14].extend([lambda: lw_weave(3, 0, "S"), lambda: finish(0, "V"), lambda: gather(1, (2,))])
+        early[15].extend([lambda: lw_quant(2)])
+        late[15].extend([lambda: lw_weave(3, 1, "S"), lambda: gather(1, (3,)), lambda: gather(3, (0, 1)), lambda: linear_and_deep(2)])
+
+        last = len(UNITS) - 1
+        for s in range(1, len(UNITS)):
+            if 0 <= s - 3:
+                total_square(s - 3)
+            if 0 <= s - 1:
+                e_square(s - 1)
+            for job in early[s]:
+                job()
+            if 0 <= s - 2:
+                e_quant(s - 2)
+            if 0 <= s - 1:
+                e_round(s - 1, "G")
+            if 0 <= s - 3:
+                subtract(s - 3)
+            if 0 <= s - 4:
+                scale(s - 4, "G")
+            if 0 <= s - 2:
+                products(s - 2)
+            if s <= last:
+                add_ids(s)
+            if s + 1 <= last:
+                embed(s + 1)
+            for job in late[s]:
+                job()
+        total_square(13)
+        e_square(15)
+        scale(12, "V")
+        e_quant(14)
+        subtract(13)
+        products(14)
+        e_round(15, "V")
+        gather(2, (2,))
+        lw_quant(3)
+        linear_and_deep(3)
+        finish(1, "S")
+        scale(13, "V")
+        total_square(14)
+        e_quant(15)
+        subtract(14)
+        products(15)
+        gather(2, (3,))
+        scale(14, "V")
+        total_square(15)
+        gather(3, (2,))
+        finish(2, "S")
+        subtract(15)
+        scale(15, "V")
+        gather(3, (3,))
+        finish(3, "S")

@@ -17,7 +17,9 @@ ALU = mybir.AluOpType
 
 P = 128
 PASS = 512
-UNITS = [(0, j) for j in range(4)] + [(1, j) for j in range(4)] + [(r, j) for j in range(4) for r in (2, 3)]
+UNITS = [(r, jt) for r in range(4) for jt in (0, 1)] + [(r, jt) for jt in (2, 3) for r in range(4)]
+
+WITH_F = (3, 3, 2, 0)
 
 
 def tile_attribute_fm_plus_mlp_f4_kernel(tc, x, attr, w_attr, ids, pair, lin, b0, u, b1, w2, out):
@@ -34,14 +36,14 @@ def tile_attribute_fm_plus_mlp_f4_kernel(tc, x, attr, w_attr, ids, pair, lin, b0
             return list(zip(tiles(name + "_c", count, [P, width], U32), tiles(name + "_s", count, [P, width], U8)))
 
         banks = [ps.tile([P, 512], F32, name="bank%d" % i) for i in range(8)]
-        e_banks, t_bank, q_bank, aux = banks[0:2], banks[2], banks[3], banks[4:8]
+        e_banks, t_bank, q_banks, f_home, acc = banks[0:2], banks[2], banks[3:5], banks[5], banks[6:8]
+        aux = banks[2:8]
+        last_acc = (acc[1], q_banks[0])
 
         attr_raw = tiles("attr_raw", 2, [P, 2048], BF16)
         x_raw = tiles("x_raw", 2, [P, 2048], BF16)
-        w_first = tiles("w_first", 2, [P, 1024], BF16)
-        ids_first = tiles("ids_first", 4, [P, 1024], BF16)
-        w_raw = tiles("w_raw", 3, [P, 2048], BF16)
-        ids_raw = tiles("ids_raw", 6, [P, 2048], BF16)
+        w_raw = tiles("w_raw", 8, [P, 1024], BF16)
+        ids_raw = tiles("ids_raw", 16, [P, 1024], BF16)
         u_raw = tiles("u_raw", 4, [P, 2048], BF16)
         lw_raw = tiles("lw_raw", 2, [P, 4096], BF16)
         vec_raw = tiles("vec_raw", 1, [P, P], BF16)[0]
@@ -51,7 +53,7 @@ def tile_attribute_fm_plus_mlp_f4_kernel(tc, x, attr, w_attr, ids, pair, lin, b0
         ident = tiles("ident", 1, [P, P], F32)[0]
         warm = tiles("warm", 2, [P, 1], F32)
 
-        stage = tiles("stage", 7, [P, 2048], BF16)
+        stage = tiles("stage", 8, [P, 2048], BF16)
         attr_q = mx_tiles("attr", 2, 512)
         x_q = mx_tiles("x", 2, 512)
         xx_q = mx_tiles("xx", 2, 512)
@@ -66,7 +68,7 @@ def tile_attribute_fm_plus_mlp_f4_kernel(tc, x, attr, w_attr, ids, pair, lin, b0
         ee_bf = tiles("ee_bf", 2, [P, 1024], BF16)
         h_bf = tiles("h_bf", 2, [P, 2048], BF16)
         tt = tiles("tt", 2, [P, 512], F32)
-        y = tiles("y", 12, [P, 512], F32)
+        y = tiles("y", 8, [P, 512], F32)
         res = tiles("res", 2, [P, 512], F32)
         used = {"stage": 0, "aux": 0}
 
@@ -102,26 +104,21 @@ def tile_attribute_fm_plus_mlp_f4_kernel(tc, x, attr, w_attr, ids, pair, lin, b0
         def half(i):
             return slice(PASS * i, PASS * (i + 1))
 
-        def load_ids(r):
-            for g in range(2):
-                load_k_first(ids_raw[2 * (r - 1) + g], ids[half(g), half(r)])
+        def load_w(h):
+            load_k_first(w_raw[h], w_attr[:, 256 * h : 256 * (h + 1)])
 
-        def load_first_ids(h):
+        def load_ids(h):
             for g in range(2):
-                load_k_first(ids_first[2 * h + g], ids[half(g), 256 * h : 256 * (h + 1)])
+                load_k_first(ids_raw[2 * h + g], ids[half(g), 256 * h : 256 * (h + 1)])
 
         def rows4(tile):
             return tile[:].rearrange("p (j c) -> p j c", j=4)
 
         def w_view(h):
-            if h < 2:
-                return rows4(w_first[h])
-            return rows4(w_raw[h // 2 - 1])[:, :, 256 * (h % 2) : 256 * (h % 2 + 1)]
+            return rows4(w_raw[h])
 
         def ids_view(r, jt, g):
-            if r == 0:
-                return rows4(ids_first[2 * (jt // 2) + g])[:, :, P * (jt % 2) : P * (jt % 2 + 1)]
-            return rows4(ids_raw[2 * (r - 1) + g])[:, :, P * jt : P * (jt + 1)]
+            return rows4(ids_raw[2 * (2 * r + jt // 2) + g])[:, :, P * (jt % 2) : P * (jt % 2 + 1)]
 
         def load_x(g):
             nc.sync.dma_start(out=x_raw[g][:].rearrange("p (s c) -> p s c", s=4), in_=x[:, half(g)].rearrange("(s p) c -> p s c", p=P))
@@ -131,26 +128,30 @@ def tile_attribute_fm_plus_mlp_f4_kernel(tc, x, attr, w_attr, ids, pair, lin, b0
                 load_k_first(u_raw[2 * gh + g], u[half(g), half(gh)])
 
         load_k_first(attr_raw[0], attr[half(0), :])
-        load_k_first(w_first[0], w_attr[:, 0:256])
         load_k_first(attr_raw[1], attr[half(1), :])
-        load_first_ids(0)
-        load_k_first(w_first[1], w_attr[:, 256:512])
+        load_w(0)
         load_x(0)
+        load_ids(0)
+        load_w(2)
         load_x(1)
-        load_first_ids(1)
         load_u(0)
+        load_ids(2)
+        load_w(4)
         nc.sync.dma_start(out=vec_raw[0:16, :], in_=pair.rearrange("(i c) -> i c", c=P))
         nc.sync.dma_start(out=vec_raw[16:20, :], in_=b0.rearrange("(i c) -> i c", c=P))
         nc.sync.dma_start(out=b1_raw[:].rearrange("p (g t) -> p g t", g=2), in_=b1.rearrange("(g p t) -> p g t", g=2, t=4))
-        load_k_first(w_raw[0], w_attr[:, half(1)])
-        load_ids(1)
         load_u(1)
-        load_k_first(w_raw[1], w_attr[:, half(2)])
-        load_k_first(w_raw[2], w_attr[:, half(3)])
-        load_ids(2)
+        load_ids(4)
+        load_w(6)
+        load_ids(6)
+        for h in (1, 3, 5, 7):
+            load_w(h)
+        load_ids(1)
         load_ids(3)
         for i, src in enumerate((lin, w2)):
             nc.sync.dma_start(out=lw_raw[i][:].rearrange("p (g c) -> p g c", g=2), in_=src.rearrange("(g p j) c -> p g (j c)", g=2, j=4))
+        load_ids(5)
+        load_ids(7)
 
         make_identity(nc, ident[:])
         nc.gpsimd.memset(vec_rows[:], 0.0)
@@ -208,7 +209,7 @@ def tile_attribute_fm_plus_mlp_f4_kernel(tc, x, attr, w_attr, ids, pair, lin, b0
 
         def hidden_mm(i):
             gh, t = divmod(i, 4)
-            bank = take(aux, "aux")
+            bank = f_home
             for g in range(2):
                 mx(bank[:], u_q[2 * gh + g], P * t, x_q[g], 0, 512, g == 0, g == 1)
             held["hb", i] = bank
@@ -241,7 +242,7 @@ def tile_attribute_fm_plus_mlp_f4_kernel(tc, x, attr, w_attr, ids, pair, lin, b0
 
         def vectors():
             nc.scalar.copy(out=vec_rows[0:20, :], in_=vec_raw[0:20, :])
-            bank = take(aux, "aux")
+            bank = acc[0]
             nc.tensor.transpose(bank[:, 0:P], vec_rows[:], ident[:])
             held["vec"] = bank
 
@@ -250,7 +251,7 @@ def tile_attribute_fm_plus_mlp_f4_kernel(tc, x, attr, w_attr, ids, pair, lin, b0
             nc.scalar.copy(out=vec[:, 16:20], in_=held["vec"][:, 16:20])
 
         def y_of(n):
-            return y[n] if n < 8 else y[8 + n % 4]
+            return y[n % len(y)]
 
         def embed(n, gs=(0, 1)):
             r, jt = UNITS[n]
@@ -269,7 +270,7 @@ def tile_attribute_fm_plus_mlp_f4_kernel(tc, x, attr, w_attr, ids, pair, lin, b0
                 )
 
         def e_round(n, eng):
-            copy(eng, e_bf[:].rearrange("p (c t) -> p c t", t=4), e32[n % 2][:].rearrange("p (t c) -> p c t", t=4))
+            copy(eng, e_bf[:].rearrange("p (c i t) -> p c t i", i=4, t=4), e32[n % 2][:].rearrange("p (t c i) -> p c t i", i=4, t=4))
 
         def e_square(n):
             nc.scalar.activation(
@@ -286,16 +287,16 @@ def tile_attribute_fm_plus_mlp_f4_kernel(tc, x, attr, w_attr, ids, pair, lin, b0
             for g in range(2):
                 mx(t_bank[:], e_q[n % 2], P * g, x_q[g], 0, 512, g == 0, g == 1)
             for g in range(2):
-                mx(q_bank[:], ee_q[n % 2], P * g, xx_q[g], 0, 512, g == 0, g == 1)
+                mx(q_banks[n % 2][:], ee_q[n % 2], P * g, xx_q[g], 0, 512, g == 0, g == 1)
 
         def total_square(n):
             nc.scalar.activation(out=tt[n % 2][:], in_=t_bank[:], func=ACT.Square)
 
         def subtract(n):
-            nc.vector.tensor_tensor(out=y_of(n)[:], in0=tt[n % 2][:], in1=q_bank[:], op=ALU.subtract)
+            nc.vector.tensor_tensor(out=y_of(n)[:], in0=tt[n % 2][:], in1=q_banks[n % 2][:], op=ALU.subtract)
 
         def f_bank(jt):
-            return e_banks[0] if jt == 3 else aux[0]
+            return f_home
 
         def linear_and_deep(jt):
             bank = f_bank(jt)
@@ -305,129 +306,163 @@ def tile_attribute_fm_plus_mlp_f4_kernel(tc, x, attr, w_attr, ids, pair, lin, b0
         def scale(n, eng):
             r, jt = UNITS[n]
             gain = vec[:, 4 * r + jt : 4 * r + jt + 1]
-            if r == 3:
+            if r == WITH_F[jt]:
                 nc.vector.scalar_tensor_tensor(out=y_of(n)[:], in0=y_of(n)[:], scalar=gain, in1=f_bank(jt)[:], op0=ALU.mult, op1=ALU.add)
             else:
-                shift = vec[:, 16 + jt : 17 + jt] if r == 2 else 0.0
+                shift = vec[:, 16 + jt : 17 + jt] if r == 1 else 0.0
                 engine = nc.vector if eng == "V" else nc.gpsimd
+                if eng == "S":
+                    nc.scalar.activation(out=y_of(n)[:], in_=y_of(n)[:], func=ACT.Identity, scale=gain, bias=shift)
+                    return
                 engine.tensor_scalar(out=y_of(n)[:], in0=y_of(n)[:], scalar1=gain, scalar2=shift, op0=ALU.mult, op1=ALU.add)
 
         def gather(jt, rs):
-            bank = aux[1 + jt % 3]
             for r in rs:
                 src = y_of(UNITS.index((r, jt)))
                 for s in range(4):
+                    width = 2 if jt == 3 else 4
+                    bank = last_acc[s // 2] if jt == 3 else acc[jt % 2]
                     nc.tensor.matmul(
-                        out=bank[:, P * s : P * (s + 1)],
+                        out=bank[:, P * (s % width) : P * (s % width + 1)],
                         lhsT=src[:, P * s : P * (s + 1)],
                         rhs=ident[:],
-                        start=(r == 0 and s == 0),
-                        stop=(r == 3 and s == 3),
+                        start=(r == 0 and s % width == 0),
+                        stop=(r == 3 and s % width == width - 1),
                         is_transpose=True,
                     )
 
         def finish(jt, eng):
-            copy(eng, res[jt % 2][:], aux[1 + jt % 3][:])
+            copy(eng, res[jt % 2][:], acc[jt % 2][:])
             nc.sync.dma_start(
                 out=out[:, P * jt : P * (jt + 1)].rearrange("(s p) c -> p s c", p=P),
                 in_=res[jt % 2][:].rearrange("p (s c) -> p s c", s=4),
             )
 
+        cols = [slice(256 * h, 256 * (h + 1)) for h in range(2)]
+        t_half, q_half = (e_banks[0], t_bank), (q_banks[1], e_banks[1])
+        n_last = len(UNITS) - 1
+
+        def last_products(h):
+            for g in range(2):
+                mx(t_half[h][:, 0:256], e_q[1], P * g, x_q[g], 256 * h, 256, g == 0, g == 1)
+            for g in range(2):
+                mx(q_half[h][:, 0:256], ee_q[1], P * g, xx_q[g], 256 * h, 256, g == 0, g == 1)
+
+        def last_square(h):
+            nc.scalar.activation(out=tt[1][:, cols[h]], in_=t_half[h][:, 0:256], func=ACT.Square)
+
+        def last_sub(h):
+            nc.vector.tensor_tensor(out=y_of(n_last)[:, cols[h]], in0=tt[1][:, cols[h]], in1=q_half[h][:, 0:256], op=ALU.subtract)
+
+        def last_scale(h):
+            nc.vector.tensor_scalar(out=y_of(n_last)[:, cols[h]], in0=y_of(n_last)[:, cols[h]], scalar1=vec[:, 15:16], scalar2=None, op0=ALU.mult)
+
+        def last_finish(h):
+            copy("SV"[h], res[1][:, cols[h]], last_acc[h][:, 0:256])
+            nc.sync.dma_start(
+                out=out[256 * h : 256 * (h + 1), P * 3 : P * 4].rearrange("(s p) c -> p s c", p=P),
+                in_=res[1][:, cols[h]].rearrange("p (s c) -> p s c", s=2),
+            )
+
         a0 = turn(attr_raw[0], "SV")
+        a1 = turn(attr_raw[1], "SS")
         w_weave(0, "V")
         quantize(attr_q[0], a0[:])
-        a1 = turn(attr_raw[1], "SV")
-        w_quant(0)
-        embed(0, (0,))
-        quantize(attr_q[1], a1[:])
-        add_ids(0, (0,))
-        embed(0, (1,))
-        embed(1, (0,))
-        w_weave(1, "S")
         held["x", 0] = turn(x_raw[0], "SS")
+        w_quant(0)
+        quantize(attr_q[1], a1[:])
+        embed(0)
+        add_ids(0, (0,))
+        quantize(x_q[0], held["x", 0][:])
         add_ids(0, (1,))
-        embed(1, (1,))
+        embed(1)
+        xx_make(0, "V")
+        w_weave(2, "S")
         early = {s: [] for s in range(20)}
+        mid = {s: [] for s in range(20)}
         late = {s: [] for s in range(20)}
         def x1_turn():
             held["x", 1] = turn(x_raw[1], "SS")
-        early[1].extend([lambda: w_quant(1), lambda: x1_turn()])
-        late[1].extend([lambda: quantize(x_q[0], held["x", 0][:]), lambda: xx_make(0, "V"), lambda: quantize(x_q[1], held["x", 1][:]), lambda: xx_make(1, "S"), lambda: quantize(xx_q[0], held["xx", 0][:])])
-        early[2].extend([lambda: u_weave(0, 0, "V"), lambda: u_weave(0, 1, "V"), lambda: quantize(xx_q[1], held["xx", 1][:])])
-        late[2].extend([lambda: u_weave(1, 0, "S"), lambda: u_weave(1, 1, "S"), lambda: vectors(), lambda: w_weave(2, "V")])
-        early[3].extend([lambda: vectors_out(), lambda: u_quant(0), lambda: u_quant(1), lambda: hidden_mm(0), lambda: w_quant(2)])
-        late[3].extend([lambda: relu(0, "V"), lambda: w_weave(3, "S"), lambda: u_weave(2, 0, "S")])
-        early[4].extend([lambda: hidden_mm(1)])
-        late[4].extend([lambda: relu(1, "V"), lambda: u_weave(2, 1, "S")])
-        early[5].extend([lambda: hidden_mm(2), lambda: w_quant(3)])
-        late[5].extend([lambda: relu(2, "V"), lambda: u_weave(3, 0, "S"), lambda: u_weave(3, 1, "S")])
-        early[6].extend([lambda: hidden_mm(3), lambda: u_quant(2)])
-        late[6].extend([lambda: relu(3, "V"), lambda: w_weave(4, "S")])
-        early[7].extend([lambda: u_quant(3), lambda: hidden_mm(4), lambda: w_quant(4)])
-        late[7].extend([lambda: relu(4, "V"), lambda: w_weave(6, "S"), lambda: h_weave(0, 0, "S")])
-        early[8].extend([lambda: hidden_mm(5), lambda: w_quant(6)])
-        late[8].extend([lambda: relu(5, "V"), lambda: h_weave(0, 1, "S")])
-        early[9].extend([lambda: hidden_mm(6)])
-        late[9].extend([lambda: relu(6, "V"), lambda: w_weave(5, "S"), lambda: lw_weave(0, 0, "S")])
-        early[10].extend([lambda: hidden_mm(7), lambda: h_quant(0)])
-        late[10].extend([lambda: relu(7, "V"), lambda: lw_weave(0, 1, "S"), lambda: w_weave(7, "S")])
-        early[11].extend([lambda: w_quant(5), lambda: lw_quant(0)])
-        late[11].extend([lambda: h_weave(1, 0, "S"), lambda: h_weave(1, 1, "S"), lambda: gather(0, (0, 1))])
-        early[12].extend([lambda: w_quant(7), lambda: h_quant(1)])
-        late[12].extend([lambda: linear_and_deep(0), lambda: lw_weave(1, 0, "S"), lambda: lw_weave(1, 1, "S"), lambda: gather(0, (2,)), lambda: gather(1, (0, 1))])
-        early[13].extend([])
-        late[13].extend([lambda: lw_weave(2, 0, "S"), lambda: lw_weave(2, 1, "S"), lambda: gather(0, (3,)), lambda: gather(2, (0, 1))])
-        early[14].extend([lambda: lw_quant(1), lambda: linear_and_deep(1)])
-        late[14].extend([lambda: lw_weave(3, 0, "S"), lambda: finish(0, "V"), lambda: gather(1, (2,))])
-        early[15].extend([lambda: lw_quant(2)])
-        late[15].extend([lambda: lw_weave(3, 1, "S"), lambda: gather(1, (3,)), lambda: gather(3, (0, 1)), lambda: linear_and_deep(2)])
+        early[1].extend([lambda: x1_turn(), lambda: w_quant(2), lambda: quantize(xx_q[0], held["xx", 0][:])])
+        late[1].extend([lambda: u_weave(0, 0, "S"), lambda: u_weave(0, 1, "S")])
+        early[2].extend([lambda: xx_make(1, "V"), lambda: quantize(x_q[1], held["x", 1][:]), lambda: quantize(xx_q[1], held["xx", 1][:])])
+        late[2].extend([lambda: u_weave(1, 0, "S"), lambda: w_weave(4, "S"), lambda: vectors()])
+        early[3].extend([lambda: vectors_out(), lambda: u_weave(1, 1, "V"), lambda: u_quant(0), lambda: w_quant(4), lambda: u_quant(1), lambda: hidden_mm(0)])
+        late[3].extend([lambda: relu(0, "V"), lambda: hidden_mm(1), lambda: u_weave(2, 0, "S"), lambda: u_weave(2, 1, "S")])
+        early[4].extend([])
+        late[4].extend([lambda: relu(1, "V"), lambda: hidden_mm(2), lambda: u_weave(3, 0, "S")])
+        early[5].extend([lambda: w_weave(6, "V"), lambda: u_quant(2), lambda: w_quant(6)])
+        late[5].extend([lambda: relu(2, "V"), lambda: scale(0, "G"), lambda: hidden_mm(3), lambda: u_weave(3, 1, "S")])
+        early[6].extend([lambda: u_quant(3)])
+        late[6].extend([lambda: relu(3, "V"), lambda: scale(1, "G"), lambda: hidden_mm(4), lambda: w_weave(1, "S"), lambda: w_weave(3, "S")])
+        early[7].extend([lambda: w_quant(1)])
+        late[7].extend([lambda: relu(4, "V"), lambda: scale(2, "G"), lambda: hidden_mm(5), lambda: w_weave(5, "S")])
+        early[8].extend([lambda: w_quant(3)])
+        late[8].extend([lambda: relu(5, "V"), lambda: scale(3, "G"), lambda: hidden_mm(6), lambda: w_weave(7, "S"), lambda: h_weave(0, 0, "S")])
+        early[9].extend([lambda: w_quant(5)])
+        late[9].extend([lambda: relu(6, "V"), lambda: scale(4, "G"), lambda: hidden_mm(7), lambda: h_weave(0, 1, "S")])
+        early[10].extend([lambda: w_quant(7)])
+        late[10].extend([lambda: relu(7, "V"), lambda: scale(5, "G"), lambda: lw_weave(0, 0, "S"), lambda: lw_weave(0, 1, "S"), lambda: gather(0, (0, 1, 2))])
+        early[11].extend([lambda: h_quant(0)])
+        late[11].extend([lambda: h_weave(1, 0, "S"), lambda: gather(1, (0, 1, 2))])
+        early[12].extend([lambda: h_weave(1, 1, "V"), lambda: lw_quant(0), lambda: h_quant(1), lambda: linear_and_deep(0)])
+        late[12].extend([lambda: lw_weave(1, 0, "S"), lambda: lw_weave(1, 1, "S")])
+        early[13].extend([lambda: lw_weave(2, 0, "V"), lambda: lw_quant(1)])
+        late[13].extend([lambda: linear_and_deep(1), lambda: scale(8, "G"), lambda: gather(0, (3,)), lambda: lw_weave(2, 1, "S"), lambda: lw_weave(3, 0, "S")])
+        early[14].extend([lambda: lw_quant(2)])
+        late[14].extend([lambda: linear_and_deep(2), lambda: scale(9, "G"), lambda: gather(1, (3,)), lambda: lw_weave(3, 1, "S"), lambda: finish(0, "S"), lambda: gather(2, (0, 1))])
+        early[15].extend([lambda: lw_quant(3)])
+        late[15].extend([lambda: linear_and_deep(3), lambda: finish(1, "S"), lambda: scale(11, "G")])
+        mid[13].extend([lambda: scale(6, "V")])
+        mid[14].extend([lambda: scale(7, "V")])
+        mid[15].extend([lambda: scale(10, "V")])
+        mid[12].extend([])
 
-        last = len(UNITS) - 1
         for s in range(1, len(UNITS)):
-            if 0 <= s - 3:
+            if s >= 3:
                 total_square(s - 3)
-            if 0 <= s - 1:
-                e_square(s - 1)
+            e_square(s - 1)
             for job in early[s]:
                 job()
-            if 0 <= s - 2:
+            if s >= 2:
                 e_quant(s - 2)
-            if 0 <= s - 1:
-                e_round(s - 1, "G")
-            if 0 <= s - 3:
-                subtract(s - 3)
-            if 0 <= s - 4:
-                scale(s - 4, "G")
-            if 0 <= s - 2:
+            e_round(s - 1, "G")
+            if s >= 4:
+                subtract(s - 4)
+            if s >= 2:
                 products(s - 2)
-            if s <= last:
-                add_ids(s)
-            if s + 1 <= last:
+            for job in mid[s]:
+                job()
+            add_ids(s)
+            if s + 1 < len(UNITS):
                 embed(s + 1)
             for job in late[s]:
                 job()
         total_square(13)
         e_square(15)
-        scale(12, "V")
+        subtract(12)
         e_quant(14)
-        subtract(13)
         products(14)
         e_round(15, "V")
-        gather(2, (2,))
-        lw_quant(3)
-        linear_and_deep(3)
-        finish(1, "S")
-        scale(13, "V")
-        total_square(14)
+        gather(2, (2, 3))
+        scale(12, "V")
+        subtract(13)
         e_quant(15)
+        total_square(14)
+        last_products(0)
+        last_products(1)
+        scale(13, "G")
         subtract(14)
-        products(15)
-        gather(2, (3,))
+        last_square(0)
+        gather(3, (0, 1))
         scale(14, "V")
-        total_square(15)
-        gather(3, (2,))
+        last_square(1)
         finish(2, "S")
-        subtract(15)
-        scale(15, "V")
+        last_sub(0)
+        gather(3, (2,))
+        last_sub(1)
+        last_scale(0)
+        last_scale(1)
         gather(3, (3,))
-        finish(3, "S")
+        last_finish(0)
+        last_finish(1)

@@ -17,9 +17,21 @@ ALU = mybir.AluOpType
 
 P = 128
 PASS = 512
-UNITS = [(r, jt) for r in range(4) for jt in (0, 1)] + [(r, jt) for jt in (2, 3) for r in range(4)]
+STRIP = 256
+HALF = M // 2
 
-WITH_F = (3, 3, 2, 0)
+UNITS = [(r, jt) for r in range(R) for jt in (0, 1)] + [(r, jt) for jt in (2, 3) for r in range(R)]
+LAST = len(UNITS) - 1
+
+HIDDEN_STEP = 3
+DEEP_STEP = HIDDEN_STEP + 8
+WITH_DEEP = (3, 3, 2, 0)
+WITH_B0 = 1
+
+
+def strip_of(unit):
+    r, jt = UNITS[unit]
+    return 2 * r + jt // 2
 
 
 def tile_attribute_fm_plus_mlp_f4_kernel(tc, x, attr, w_attr, ids, pair, lin, b0, u, b1, w2, out):
@@ -29,106 +41,106 @@ def tile_attribute_fm_plus_mlp_f4_kernel(tc, x, attr, w_attr, ids, pair, lin, b0
         ps = ctx.enter_context(tc.psum_pool(name="ps", bufs=1))
         ctx.enter_context(tc.manual_schedule())
 
-        def tiles(name, count, shape, dtype):
-            return [sb.tile(shape, dtype, name="%s%d" % (name, i), align_bytes=64) for i in range(count)]
+        def tiles(name, count, width, dtype):
+            return [sb.tile([P, width], dtype, name="%s%d" % (name, i), align_bytes=64) for i in range(count)]
 
         def mx_tiles(name, count, width):
-            return list(zip(tiles(name + "_c", count, [P, width], U32), tiles(name + "_s", count, [P, width], U8)))
+            return list(zip(tiles(name + "_c", count, width, U32), tiles(name + "_s", count, width, U8)))
 
-        banks = [ps.tile([P, 512], F32, name="bank%d" % i) for i in range(8)]
-        e_banks, t_bank, q_banks, f_home, acc = banks[0:2], banks[2], banks[3:5], banks[5], banks[6:8]
-        aux = banks[2:8]
-        last_acc = (acc[1], q_banks[0])
+        banks = [ps.tile([P, PASS], F32, name="bank%d" % i) for i in range(8)]
+        e_banks, total_bank, square_banks, deep_bank, sum_banks = banks[0:2], banks[2], banks[3:5], banks[5], banks[6:8]
+        turn_banks = banks[2:8]
 
-        attr_raw = tiles("attr_raw", 2, [P, 2048], BF16)
-        x_raw = tiles("x_raw", 2, [P, 2048], BF16)
-        w_raw = tiles("w_raw", 8, [P, 1024], BF16)
-        ids_raw = tiles("ids_raw", 16, [P, 1024], BF16)
-        u_raw = tiles("u_raw", 4, [P, 2048], BF16)
-        lw_raw = tiles("lw_raw", 2, [P, 4096], BF16)
-        vec_raw = tiles("vec_raw", 1, [P, P], BF16)[0]
-        vec_rows = tiles("vec_rows", 1, [P, P], F32)[0]
-        vec = tiles("vec", 1, [P, 20], F32)[0]
-        b1_raw = tiles("b1_raw", 1, [P, 8], BF16)[0]
-        ident = tiles("ident", 1, [P, P], F32)[0]
-        warm = tiles("warm", 2, [P, 1], F32)
+        attr_raw = tiles("attr_raw", 2, 4 * K, BF16)
+        x_raw = tiles("x_raw", 2, 4 * PASS, BF16)
+        w_raw = tiles("w_raw", D // STRIP, 4 * STRIP, BF16)
+        ids_raw = tiles("ids_raw", 2 * D // STRIP, 4 * STRIP, BF16)
+        u_raw = tiles("u_raw", 4, 4 * PASS, BF16)
+        lin_w2_raw = tiles("lin_w2_raw", 2, 8 * T, BF16)
+        vec_raw = tiles("vec_raw", 1, P, BF16)[0]
+        vec_rows = tiles("vec_rows", 1, P, F32)[0]
+        gains = tiles("gains", 1, D // P, F32)[0]
+        b0_cols = tiles("b0_cols", 1, T // P, F32)[0]
+        b1_slots = tiles("b1_slots", 1, 8, BF16)[0]
+        ident = tiles("ident", 1, P, F32)[0]
 
-        stage = tiles("stage", 8, [P, 2048], BF16)
-        attr_q = mx_tiles("attr", 2, 512)
-        x_q = mx_tiles("x", 2, 512)
-        xx_q = mx_tiles("xx", 2, 512)
-        w_q = mx_tiles("w", 8, 256)
-        u_q = mx_tiles("u", 4, 512)
-        h_q = mx_tiles("h", 2, 512)
-        lw_q = mx_tiles("lw", 4, 512)
-        e_q = mx_tiles("e", 2, 256)
-        ee_q = mx_tiles("ee", 2, 256)
-        e32 = tiles("e32", 2, [P, 1024], F32)
-        e_bf = tiles("e_bf", 1, [P, 1024], BF16)[0]
-        ee_bf = tiles("ee_bf", 2, [P, 1024], BF16)
-        h_bf = tiles("h_bf", 2, [P, 2048], BF16)
-        tt = tiles("tt", 2, [P, 512], F32)
-        y = tiles("y", 8, [P, 512], F32)
-        res = tiles("res", 2, [P, 512], F32)
-        used = {"stage": 0, "aux": 0}
+        woven = tiles("woven", 10, 4 * PASS, BF16)
+        attr_q = mx_tiles("attr", 2, PASS)
+        x_q = mx_tiles("x", 2, M)
+        xx_q = mx_tiles("xx", 2, M)
+        w_q = mx_tiles("w", D // STRIP, STRIP)
+        u_q = mx_tiles("u", 4, PASS)
+        hidden_q = mx_tiles("hidden", 2, M)
+        lin_w2_q = mx_tiles("lin_w2", 4, 4 * P)
+        e_q = mx_tiles("e", 2, 2 * P)
+        ee_q = mx_tiles("ee", 2, 2 * P)
+        e32 = tiles("e32", 2, 8 * P, F32)
+        e_bf = tiles("e_bf", 1, 8 * P, BF16)[0]
+        ee_bf = tiles("ee_bf", 2, 8 * P, BF16)
+        total_sq = tiles("total_sq", 2, M, F32)
+        terms = tiles("terms", 8, M, F32)
+        result = tiles("result", 2, M, F32)
+        taken = {"woven": 0, "turn": 0}
+        held = {}
 
         def take(ring, name):
-            used[name] = used[name] + 1
-            return ring[(used[name] - 1) % len(ring)]
+            taken[name] = taken[name] + 1
+            return ring[(taken[name] - 1) % len(ring)]
 
-        def copy(eng, dst, src):
-            if eng == "S":
-                nc.scalar.copy(out=dst, in_=src)
-            elif eng == "V":
-                nc.vector.tensor_copy(out=dst, in_=src)
-            else:
-                nc.gpsimd.tensor_scalar(out=dst, in0=src, scalar1=1.0, scalar2=0.0, op0=ALU.mult, op1=ALU.add)
+        def on_scalar(dst, src):
+            nc.scalar.copy(out=dst, in_=src)
+
+        def on_vector(dst, src):
+            nc.vector.tensor_copy(out=dst, in_=src)
 
         def quantize(q, src):
             nc.vector.quantize_mx(out=q[0][:].bitcast(FP8X4), scales=q[1][:], in_=src)
 
-        def mx(dst, lhs, lcol, rhs, rcol, n, start, stop):
+        def mx(dst, lhs, lhs_col, rhs, rhs_col, n, start, stop):
             nc.tensor.matmul_mx(
                 out=dst,
-                lhsT=lhs[0][:, lcol : lcol + P].bitcast(FP8X4),
-                lhsT_scale=lhs[1][:, lcol : lcol + P],
-                rhs=rhs[0][:, rcol : rcol + n].bitcast(FP8X4),
-                rhs_scale=rhs[1][:, rcol : rcol + n],
+                lhsT=lhs[0][:, lhs_col : lhs_col + P].bitcast(FP8X4),
+                lhsT_scale=lhs[1][:, lhs_col : lhs_col + P],
+                rhs=rhs[0][:, rhs_col : rhs_col + n].bitcast(FP8X4),
+                rhs_scale=rhs[1][:, rhs_col : rhs_col + n],
                 start=start,
                 stop=stop,
             )
 
-        def load_k_first(dst, src):
-            nc.sync.dma_start(out=dst[:].rearrange("p (j c) -> p j c", j=4), in_=src.rearrange("(p j) c -> p j c", j=4))
+        def part(i, width):
+            return slice(width * i, width * (i + 1))
 
-        def half(i):
-            return slice(PASS * i, PASS * (i + 1))
+        def slots(tile):
+            return tile[:].rearrange("p (t c) -> p t c", t=4)
 
-        def load_w(h):
-            load_k_first(w_raw[h], w_attr[:, 256 * h : 256 * (h + 1)])
+        def walk_woven(ap):
+            return ap.rearrange("p (c i t) -> p c t i", i=4, t=4)
 
-        def load_ids(h):
-            for g in range(2):
-                load_k_first(ids_raw[2 * h + g], ids[half(g), 256 * h : 256 * (h + 1)])
+        def walk_slots(ap):
+            return ap.rearrange("p t (c i) -> p c t i", i=4)
 
-        def rows4(tile):
-            return tile[:].rearrange("p (j c) -> p j c", j=4)
-
-        def w_view(h):
-            return rows4(w_raw[h])
-
-        def ids_view(r, jt, g):
-            return rows4(ids_raw[2 * (2 * r + jt // 2) + g])[:, :, P * (jt % 2) : P * (jt % 2 + 1)]
+        def load_rows(dst, src):
+            nc.sync.dma_start(out=slots(dst), in_=src.rearrange("(p t) c -> p t c", t=4))
 
         def load_x(g):
-            nc.sync.dma_start(out=x_raw[g][:].rearrange("p (s c) -> p s c", s=4), in_=x[:, half(g)].rearrange("(s p) c -> p s c", p=P))
+            nc.sync.dma_start(
+                out=x_raw[g][:].rearrange("p (s c) -> p s c", s=4),
+                in_=x[:, part(g, PASS)].rearrange("(s p) c -> p s c", p=P),
+            )
+
+        def load_w(strip):
+            load_rows(w_raw[strip], w_attr[:, part(strip, STRIP)])
+
+        def load_ids(strip):
+            for g in range(2):
+                load_rows(ids_raw[2 * strip + g], ids[part(g, PASS), part(strip, STRIP)])
 
         def load_u(gh):
             for g in range(2):
-                load_k_first(u_raw[2 * gh + g], u[half(g), half(gh)])
+                load_rows(u_raw[2 * gh + g], u[part(g, PASS), part(gh, PASS)])
 
-        load_k_first(attr_raw[0], attr[half(0), :])
-        load_k_first(attr_raw[1], attr[half(1), :])
+        load_rows(attr_raw[0], attr[part(0, PASS), :])
+        load_rows(attr_raw[1], attr[part(1, PASS), :])
         load_w(0)
         load_x(0)
         load_ids(0)
@@ -137,332 +149,338 @@ def tile_attribute_fm_plus_mlp_f4_kernel(tc, x, attr, w_attr, ids, pair, lin, b0
         load_u(0)
         load_ids(2)
         load_w(4)
+        load_w(6)
         nc.sync.dma_start(out=vec_raw[0:16, :], in_=pair.rearrange("(i c) -> i c", c=P))
         nc.sync.dma_start(out=vec_raw[16:20, :], in_=b0.rearrange("(i c) -> i c", c=P))
-        nc.sync.dma_start(out=b1_raw[:].rearrange("p (g t) -> p g t", g=2), in_=b1.rearrange("(g p t) -> p g t", g=2, t=4))
+        nc.sync.dma_start(
+            out=b1_slots[:].rearrange("p (g t) -> p g t", g=2), in_=b1.rearrange("(g p t) -> p g t", g=2, t=4)
+        )
         load_u(1)
         load_ids(4)
-        load_w(6)
         load_ids(6)
-        for h in (1, 3, 5, 7):
-            load_w(h)
+        for strip in (1, 3, 5, 7):
+            load_w(strip)
         load_ids(1)
         load_ids(3)
-        for i, src in enumerate((lin, w2)):
-            nc.sync.dma_start(out=lw_raw[i][:].rearrange("p (g c) -> p g c", g=2), in_=src.rearrange("(g p j) c -> p g (j c)", g=2, j=4))
+        for raw, src in zip(lin_w2_raw, (lin, w2)):
+            nc.sync.dma_start(
+                out=raw[:].rearrange("p (g c) -> p g c", g=2), in_=src.rearrange("(g p t) c -> p g (t c)", g=2, t=4)
+            )
         load_ids(5)
         load_ids(7)
 
-        make_identity(nc, ident[:])
-        nc.gpsimd.memset(vec_rows[:], 0.0)
-        nc.vector.memset(warm[0][:], 0.0)
-        nc.scalar.activation(out=warm[1][:], in_=warm[0][:], func=ACT.Square)
-
-        def turn(raw, engs):
+        def turn(raw, b, key):
             words = raw[:].bitcast(F32)
-            dst = take(stage, "stage")
-            dwords = dst[:].bitcast(F32)
+            bank = take(turn_banks, "turn")
+            for s in range(2):
+                for w in range(2):
+                    first = 256 * (2 * b + s)
+                    nc.tensor.transpose(bank[:, part(2 * s + w, P)], words[:, first + w : first + 256 : 2], ident[:])
+            if b == 0:
+                held[key] = take(woven, "woven")
+            held[key, b] = bank
+
+        def turn_out(key, b, copy):
+            copy(
+                held[key][:].bitcast(F32)[:, part(b, PASS)].rearrange("p (s m w) -> p s m w", s=2, w=2),
+                held[key, b][:].rearrange("p (s w m) -> p s m w", s=2, w=2),
+            )
+
+        def turn_both(raw, key, copies):
             for b in range(2):
-                bank = take(aux, "aux")
-                for s in range(2):
-                    for w in range(2):
-                        first = 256 * (2 * b + s)
-                        nc.tensor.transpose(bank[:, P * (2 * s + w) : P * (2 * s + w + 1)], words[:, first + w : first + 256 : 2], ident[:])
-                copy(
-                    engs[b],
-                    dwords[:, 512 * b : 512 * (b + 1)].rearrange("p (s m w) -> p s m w", s=2, w=2),
-                    bank[:].rearrange("p (s w m) -> p s m w", s=2, w=2),
-                )
-            return dst
+                turn(raw, b, key)
+                turn_out(key, b, copies[b])
 
-        def weave(eng, dst, src):
-            copy(eng, dst.rearrange("p (c i j) -> p c j i", i=4, j=4), src.rearrange("p j (c i) -> p c j i", i=4))
+        def weave_w(strip, copy):
+            held["w", strip] = take(woven, "woven")
+            copy(walk_woven(held["w", strip][:, 0 : 4 * STRIP]), walk_slots(slots(w_raw[strip])))
 
-        held = {}
+        def quantize_w(strip):
+            quantize(w_q[strip], held["w", strip][:, 0 : 4 * STRIP])
 
-        def w_weave(h, eng):
-            dst = take(stage, "stage")
-            weave(eng, dst[:, 0:1024], w_view(h))
-            held["w", h] = dst
+        def weave_u(i, piece, copy):
+            if piece == 0:
+                held["u", i] = take(woven, "woven")
+            copy(
+                held["u", i][:].rearrange("p (v m t) -> p m t v", v=4, t=4)[:, part(piece, 64)],
+                u_raw[i][:].rearrange("p (t m v) -> p m t v", t=4, v=4)[:, part(piece, 64)],
+            )
 
-        def w_quant(h):
-            quantize(w_q[h], held["w", h][:, 0:1024])
+        def weave_lin_w2(jt, piece, copy):
+            if piece == 0:
+                held["lin_w2", jt] = take(woven, "woven")
+            src = lin_w2_raw[piece][:].rearrange("p (g t c) -> p g t c", g=2, t=4)[:, :, :, part(jt, P)]
+            copy(
+                held["lin_w2", jt][:, part(piece, 8 * P)].rearrange("p (g c i t) -> p g c t i", g=2, i=4, t=4),
+                src.rearrange("p g t (c i) -> p g c t i", i=4),
+            )
 
-        def u_weave(i, part, eng):
-            if part == 0:
-                held["u", i] = take(stage, "stage")
-            ms = slice(64 * part, 64 * (part + 1))
-            copy(eng, held["u", i][:].rearrange("p (t m j) -> p m j t", t=4, j=4)[:, ms], u_raw[i][:].rearrange("p (j m t) -> p m j t", j=4, t=4)[:, ms])
-
-        def u_quant(i):
-            quantize(u_q[i], held["u", i][:])
-
-        def lw_weave(jt, which, eng):
-            if which == 0:
-                held["lw", jt] = take(stage, "stage")
-            dst = held["lw", jt][:, 1024 * which : 1024 * (which + 1)]
-            src = lw_raw[which][:].rearrange("p (g j c) -> p g j c", g=2, j=4)[:, :, :, P * jt : P * (jt + 1)]
-            copy(eng, dst.rearrange("p (g c i j) -> p g c j i", g=2, i=4, j=4), src.rearrange("p g j (c i) -> p g c j i", i=4))
-
-        def lw_quant(jt):
-            quantize(lw_q[jt], held["lw", jt][:])
-
-        def hidden_mm(i):
-            gh, t = divmod(i, 4)
-            bank = f_home
-            for g in range(2):
-                mx(bank[:], u_q[2 * gh + g], P * t, x_q[g], 0, 512, g == 0, g == 1)
-            held["hb", i] = bank
-
-        def relu(i, eng):
-            gh, t = divmod(i, 4)
-            bank = held["hb", i]
-            dst = h_bf[gh][:, 512 * t : 512 * (t + 1)]
-            if eng == "S":
-                nc.scalar.activation(out=dst, in_=bank[:], func=ACT.Relu, bias=b1_raw[:, i : i + 1])
-            else:
-                nc.vector.tensor_scalar(out=dst, in0=bank[:], scalar1=b1_raw[:, i : i + 1], scalar2=0.0, op0=ALU.add, op1=ALU.max)
-
-        def h_weave(gh, part, eng):
-            if part == 0:
-                held["h", gh] = take(stage, "stage")
-            src = h_bf[gh][:].rearrange("p (j c) -> p j c", j=4)
-            weave(eng, held["h", gh][:, 1024 * part : 1024 * (part + 1)], src[:, :, 256 * part : 256 * (part + 1)])
-
-        def h_quant(gh):
-            quantize(h_q[gh], held["h", gh][:])
-
-        def xx_make(g, eng):
-            dst = take(stage, "stage")
-            if eng == "S":
-                nc.scalar.activation(out=dst[:], in_=held["x", g][:], func=ACT.Square)
-            else:
-                nc.vector.tensor_tensor(out=dst[:], in0=held["x", g][:], in1=held["x", g][:], op=ALU.mult)
-            held["xx", g] = dst
-
-        def vectors():
+        def turn_vectors():
             nc.scalar.copy(out=vec_rows[0:20, :], in_=vec_raw[0:20, :])
-            bank = acc[0]
-            nc.tensor.transpose(bank[:, 0:P], vec_rows[:], ident[:])
-            held["vec"] = bank
+            nc.tensor.transpose(sum_banks[0][:, 0:P], vec_rows[:], ident[:])
 
         def vectors_out():
-            nc.scalar.activation(out=vec[:, 0:16], in_=held["vec"][:, 0:16], func=ACT.Copy, scale=0.5)
-            nc.scalar.copy(out=vec[:, 16:20], in_=held["vec"][:, 16:20])
+            nc.scalar.activation(out=gains[:], in_=sum_banks[0][:, 0:16], func=ACT.Copy, scale=0.5)
+            nc.scalar.copy(out=b0_cols[:], in_=sum_banks[0][:, 16:20])
 
-        def y_of(n):
-            return y[n % len(y)]
+        def hidden_matmuls(i):
+            gh, s = divmod(i, 4)
+            for v in range(4):
+                for g in range(2):
+                    mx(deep_bank[:, part(v, P)], u_q[2 * gh + g], P * v, x_q[g], P * s, P, g == 0, g == 1)
 
-        def embed(n, gs=(0, 1)):
-            r, jt = UNITS[n]
-            for g in gs:
+        def hidden_bias(i):
+            gh, s = divmod(i, 4)
+            if s == 0:
+                held["hidden", gh] = take(woven, "woven")
+            nc.vector.tensor_tensor(
+                out=held["hidden", gh][:, part(s, PASS)].rearrange("p (m v) -> p m v", v=4),
+                in0=deep_bank[:].rearrange("p (v m) -> p m v", v=4),
+                in1=b1_slots[:, part(gh, 4)].unsqueeze(1).to_broadcast([P, P, 4]),
+                op=ALU.add,
+            )
+
+        def relu(gh):
+            tile = held["hidden", gh]
+            nc.vector.tensor_scalar(out=tile[:], in0=tile[:], scalar1=0.0, scalar2=None, op0=ALU.max)
+
+        def first_and_deep(jt):
+            for i, rhs in enumerate(x_q + hidden_q):
+                mx(deep_bank[:], lin_w2_q[jt], P * i, rhs, 0, M, i == 0, i == 3)
+
+        def embed(n, passes=(0, 1)):
+            for g in passes:
                 for t in range(4):
-                    mx(e_banks[g][:, P * t : P * (t + 1)], attr_q[g], P * t, w_q[2 * r + jt // 2], P * (jt % 2), P, True, True)
+                    mx(e_banks[g][:, part(t, P)], attr_q[g], P * t, w_q[strip_of(n)], P * (UNITS[n][1] % 2), P, True, True)
 
-        def add_ids(n, gs=(0, 1)):
-            r, jt = UNITS[n]
-            for g in gs:
+        def add_ids(n, passes=(0, 1)):
+            for g in passes:
                 nc.vector.tensor_tensor(
                     out=e32[n % 2][:].rearrange("p (t g c) -> p t g c", t=4, g=2)[:, :, g, :],
-                    in0=e_banks[g][:].rearrange("p (t c) -> p t c", t=4),
-                    in1=ids_view(r, jt, g),
+                    in0=slots(e_banks[g]),
+                    in1=slots(ids_raw[2 * strip_of(n) + g])[:, :, part(UNITS[n][1] % 2, P)],
                     op=ALU.add,
                 )
 
-        def e_round(n, eng):
-            copy(eng, e_bf[:].rearrange("p (c i t) -> p c t i", i=4, t=4), e32[n % 2][:].rearrange("p (t c i) -> p c t i", i=4, t=4))
-
-        def e_square(n):
-            nc.scalar.activation(
-                out=ee_bf[n % 2][:].rearrange("p (c i t) -> p c t i", i=4, t=4),
-                in_=e32[n % 2][:].rearrange("p (t c i) -> p c t i", i=4, t=4),
-                func=ACT.Square,
+        def round_e(n):
+            nc.gpsimd.tensor_scalar(
+                out=walk_woven(e_bf[:]), in0=walk_slots(slots(e32[n % 2])), scalar1=1.0, scalar2=0.0, op0=ALU.mult, op1=ALU.add
             )
 
-        def e_quant(n):
+        def square_e(n):
+            nc.scalar.activation(out=walk_woven(ee_bf[n % 2][:]), in_=walk_slots(slots(e32[n % 2])), func=ACT.Square)
+
+        def quantize_e(n):
             quantize(e_q[n % 2], e_bf[:])
             quantize(ee_q[n % 2], ee_bf[n % 2][:])
 
-        def products(n):
+        def products(n, to_total, to_squares, first_sample, samples):
             for g in range(2):
-                mx(t_bank[:], e_q[n % 2], P * g, x_q[g], 0, 512, g == 0, g == 1)
+                mx(to_total[:, 0:samples], e_q[n % 2], P * g, x_q[g], first_sample, samples, g == 0, g == 1)
             for g in range(2):
-                mx(q_banks[n % 2][:], ee_q[n % 2], P * g, xx_q[g], 0, 512, g == 0, g == 1)
+                mx(to_squares[:, 0:samples], ee_q[n % 2], P * g, xx_q[g], first_sample, samples, g == 0, g == 1)
 
-        def total_square(n):
-            nc.scalar.activation(out=tt[n % 2][:], in_=t_bank[:], func=ACT.Square)
+        def whole_products(n):
+            products(n, total_bank, square_banks[n % 2], 0, M)
+
+        def square_total(n):
+            nc.scalar.activation(out=total_sq[n % 2][:], in_=total_bank[:], func=ACT.Square)
+
+        def term(n):
+            return terms[n % len(terms)]
 
         def subtract(n):
-            nc.vector.tensor_tensor(out=y_of(n)[:], in0=tt[n % 2][:], in1=q_banks[n % 2][:], op=ALU.subtract)
+            nc.vector.tensor_tensor(out=term(n)[:], in0=total_sq[n % 2][:], in1=square_banks[n % 2][:], op=ALU.subtract)
 
-        def f_bank(jt):
-            return f_home
-
-        def linear_and_deep(jt):
-            bank = f_bank(jt)
-            for i, rhs in enumerate(x_q + h_q):
-                mx(bank[:], lw_q[jt], P * i, rhs, 0, 512, i == 0, i == 3)
-
-        def scale(n, eng):
+        def gain(n):
             r, jt = UNITS[n]
-            gain = vec[:, 4 * r + jt : 4 * r + jt + 1]
-            if r == WITH_F[jt]:
-                nc.vector.scalar_tensor_tensor(out=y_of(n)[:], in0=y_of(n)[:], scalar=gain, in1=f_bank(jt)[:], op0=ALU.mult, op1=ALU.add)
-            else:
-                shift = vec[:, 16 + jt : 17 + jt] if r == 1 else 0.0
-                engine = nc.vector if eng == "V" else nc.gpsimd
-                if eng == "S":
-                    nc.scalar.activation(out=y_of(n)[:], in_=y_of(n)[:], func=ACT.Identity, scale=gain, bias=shift)
-                    return
-                engine.tensor_scalar(out=y_of(n)[:], in0=y_of(n)[:], scalar1=gain, scalar2=shift, op0=ALU.mult, op1=ALU.add)
+            return gains[:, part(4 * r + jt, 1)]
 
-        def gather(jt, rs):
-            for r in rs:
-                src = y_of(UNITS.index((r, jt)))
+        def scale_on_gpsimd(n):
+            r, jt = UNITS[n]
+            shift = b0_cols[:, part(jt, 1)] if r == WITH_B0 else 0.0
+            nc.gpsimd.tensor_scalar(out=term(n)[:], in0=term(n)[:], scalar1=gain(n), scalar2=shift, op0=ALU.mult, op1=ALU.add)
+
+        def scale_on_scalar(n, cols=slice(0, M)):
+            r, jt = UNITS[n]
+            shift = b0_cols[:, part(jt, 1)] if r == WITH_B0 else 0.0
+            nc.scalar.activation(out=term(n)[:, cols], in_=term(n)[:, cols], func=ACT.Identity, scale=gain(n), bias=shift)
+
+        def scale_with_deep(jt):
+            n = UNITS.index((WITH_DEEP[jt], jt))
+            nc.vector.scalar_tensor_tensor(
+                out=term(n)[:], in0=term(n)[:], scalar=gain(n), in1=deep_bank[:], op0=ALU.mult, op1=ALU.add
+            )
+
+        last_sum_banks = (sum_banks[1], square_banks[0])
+
+        def gather(jt, components):
+            width = 2 if jt == 3 else 4
+            for r in components:
                 for s in range(4):
-                    width = 2 if jt == 3 else 4
-                    bank = last_acc[s // 2] if jt == 3 else acc[jt % 2]
+                    bank = last_sum_banks[s // 2] if jt == 3 else sum_banks[jt % 2]
                     nc.tensor.matmul(
-                        out=bank[:, P * (s % width) : P * (s % width + 1)],
-                        lhsT=src[:, P * s : P * (s + 1)],
+                        out=bank[:, part(s % width, P)],
+                        lhsT=term(UNITS.index((r, jt)))[:, part(s, P)],
                         rhs=ident[:],
                         start=(r == 0 and s % width == 0),
-                        stop=(r == 3 and s % width == width - 1),
+                        stop=(r == R - 1 and s % width == width - 1),
                         is_transpose=True,
                     )
 
-        def finish(jt, eng):
-            copy(eng, res[jt % 2][:], acc[jt % 2][:])
+        def store(jt, bank, first_sample, samples, copy):
+            staged = result[jt % 2][:, first_sample : first_sample + samples]
+            copy(staged, bank[:, 0:samples])
             nc.sync.dma_start(
-                out=out[:, P * jt : P * (jt + 1)].rearrange("(s p) c -> p s c", p=P),
-                in_=res[jt % 2][:].rearrange("p (s c) -> p s c", s=4),
+                out=out[first_sample : first_sample + samples, part(jt, P)].rearrange("(s p) c -> p s c", p=P),
+                in_=staged.rearrange("p (s c) -> p s c", c=P),
             )
 
-        cols = [slice(256 * h, 256 * (h + 1)) for h in range(2)]
-        t_half, q_half = (e_banks[0], t_bank), (q_banks[1], e_banks[1])
-        n_last = len(UNITS) - 1
-
-        def last_products(h):
-            for g in range(2):
-                mx(t_half[h][:, 0:256], e_q[1], P * g, x_q[g], 256 * h, 256, g == 0, g == 1)
-            for g in range(2):
-                mx(q_half[h][:, 0:256], ee_q[1], P * g, xx_q[g], 256 * h, 256, g == 0, g == 1)
-
-        def last_square(h):
-            nc.scalar.activation(out=tt[1][:, cols[h]], in_=t_half[h][:, 0:256], func=ACT.Square)
-
-        def last_sub(h):
-            nc.vector.tensor_tensor(out=y_of(n_last)[:, cols[h]], in0=tt[1][:, cols[h]], in1=q_half[h][:, 0:256], op=ALU.subtract)
-
-        def last_scale(h):
-            nc.vector.tensor_scalar(out=y_of(n_last)[:, cols[h]], in0=y_of(n_last)[:, cols[h]], scalar1=vec[:, 15:16], scalar2=None, op0=ALU.mult)
-
-        def last_finish(h):
-            copy("SV"[h], res[1][:, cols[h]], last_acc[h][:, 0:256])
-            nc.sync.dma_start(
-                out=out[256 * h : 256 * (h + 1), P * 3 : P * 4].rearrange("(s p) c -> p s c", p=P),
-                in_=res[1][:, cols[h]].rearrange("p (s c) -> p s c", s=2),
-            )
-
-        a0 = turn(attr_raw[0], "SV")
-        a1 = turn(attr_raw[1], "SS")
-        w_weave(0, "V")
-        quantize(attr_q[0], a0[:])
-        held["x", 0] = turn(x_raw[0], "SS")
-        w_quant(0)
-        quantize(attr_q[1], a1[:])
+        make_identity(nc, ident[:])
+        nc.scalar.activation(out=vec_rows[:], in_=ident[:], func=ACT.Square, scale=0.0)
+        turn_both(attr_raw[0], "attr0", (on_scalar, on_vector))
+        turn_both(attr_raw[1], "attr1", (on_scalar, on_scalar))
+        weave_w(strip_of(0), on_vector)
+        quantize(attr_q[0], held["attr0"][:])
+        turn_both(x_raw[0], "x0", (on_scalar, on_scalar))
+        quantize_w(strip_of(0))
+        quantize(attr_q[1], held["attr1"][:])
         embed(0)
         add_ids(0, (0,))
-        quantize(x_q[0], held["x", 0][:])
+        embed(1, (0,))
+        quantize(x_q[0], held["x0"][:])
+        held["xx0"] = take(woven, "woven")
+        nc.scalar.activation(out=held["xx0"][:], in_=held["x0"][:], func=ACT.Square)
+        weave_w(strip_of(2), on_vector)
+        turn(x_raw[1], 0, "x1")
+        turn_out("x1", 0, on_scalar)
+        turn(x_raw[1], 1, "x1")
+        quantize_w(strip_of(2))
         add_ids(0, (1,))
-        embed(1)
-        xx_make(0, "V")
-        w_weave(2, "S")
-        early = {s: [] for s in range(20)}
-        mid = {s: [] for s in range(20)}
-        late = {s: [] for s in range(20)}
-        def x1_turn():
-            held["x", 1] = turn(x_raw[1], "SS")
-        early[1].extend([lambda: x1_turn(), lambda: w_quant(2), lambda: quantize(xx_q[0], held["xx", 0][:])])
-        late[1].extend([lambda: u_weave(0, 0, "S"), lambda: u_weave(0, 1, "S")])
-        early[2].extend([lambda: xx_make(1, "V"), lambda: quantize(x_q[1], held["x", 1][:]), lambda: quantize(xx_q[1], held["xx", 1][:])])
-        late[2].extend([lambda: u_weave(1, 0, "S"), lambda: w_weave(4, "S"), lambda: vectors()])
-        early[3].extend([lambda: vectors_out(), lambda: u_weave(1, 1, "V"), lambda: u_quant(0), lambda: w_quant(4), lambda: u_quant(1), lambda: hidden_mm(0)])
-        late[3].extend([lambda: relu(0, "V"), lambda: hidden_mm(1), lambda: u_weave(2, 0, "S"), lambda: u_weave(2, 1, "S")])
-        early[4].extend([])
-        late[4].extend([lambda: relu(1, "V"), lambda: hidden_mm(2), lambda: u_weave(3, 0, "S")])
-        early[5].extend([lambda: w_weave(6, "V"), lambda: u_quant(2), lambda: w_quant(6)])
-        late[5].extend([lambda: relu(2, "V"), lambda: scale(0, "G"), lambda: hidden_mm(3), lambda: u_weave(3, 1, "S")])
-        early[6].extend([lambda: u_quant(3)])
-        late[6].extend([lambda: relu(3, "V"), lambda: scale(1, "G"), lambda: hidden_mm(4), lambda: w_weave(1, "S"), lambda: w_weave(3, "S")])
-        early[7].extend([lambda: w_quant(1)])
-        late[7].extend([lambda: relu(4, "V"), lambda: scale(2, "G"), lambda: hidden_mm(5), lambda: w_weave(5, "S")])
-        early[8].extend([lambda: w_quant(3)])
-        late[8].extend([lambda: relu(5, "V"), lambda: scale(3, "G"), lambda: hidden_mm(6), lambda: w_weave(7, "S"), lambda: h_weave(0, 0, "S")])
-        early[9].extend([lambda: w_quant(5)])
-        late[9].extend([lambda: relu(6, "V"), lambda: scale(4, "G"), lambda: hidden_mm(7), lambda: h_weave(0, 1, "S")])
-        early[10].extend([lambda: w_quant(7)])
-        late[10].extend([lambda: relu(7, "V"), lambda: scale(5, "G"), lambda: lw_weave(0, 0, "S"), lambda: lw_weave(0, 1, "S"), lambda: gather(0, (0, 1, 2))])
-        early[11].extend([lambda: h_quant(0)])
-        late[11].extend([lambda: h_weave(1, 0, "S"), lambda: gather(1, (0, 1, 2))])
-        early[12].extend([lambda: h_weave(1, 1, "V"), lambda: lw_quant(0), lambda: h_quant(1), lambda: linear_and_deep(0)])
-        late[12].extend([lambda: lw_weave(1, 0, "S"), lambda: lw_weave(1, 1, "S")])
-        early[13].extend([lambda: lw_weave(2, 0, "V"), lambda: lw_quant(1)])
-        late[13].extend([lambda: linear_and_deep(1), lambda: scale(8, "G"), lambda: gather(0, (3,)), lambda: lw_weave(2, 1, "S"), lambda: lw_weave(3, 0, "S")])
-        early[14].extend([lambda: lw_quant(2)])
-        late[14].extend([lambda: linear_and_deep(2), lambda: scale(9, "G"), lambda: gather(1, (3,)), lambda: lw_weave(3, 1, "S"), lambda: finish(0, "S"), lambda: gather(2, (0, 1))])
-        early[15].extend([lambda: lw_quant(3)])
-        late[15].extend([lambda: linear_and_deep(3), lambda: finish(1, "S"), lambda: scale(11, "G")])
-        mid[13].extend([lambda: scale(6, "V")])
-        mid[14].extend([lambda: scale(7, "V")])
-        mid[15].extend([lambda: scale(10, "V")])
-        mid[12].extend([])
+        embed(1, (1,))
+        weave_u(0, 0, on_scalar)
+        square_e(0)
+        round_e(0)
+        add_ids(1, (0,))
+        turn_out("x1", 1, on_vector)
+        add_ids(1, (1,))
+        embed(2)
+        weave_u(0, 1, on_scalar)
 
-        for s in range(1, len(UNITS)):
+        def w_job(strip):
+            due = [strip_of(n) for n in range(len(UNITS))].index(strip) - 1
+            return (due, [lambda: weave_w(strip, on_scalar)], [], lambda: quantize_w(strip))
+
+        def u_job(i):
+            due = HIDDEN_STEP + 4 * (i // 2)
+            pieces = [lambda: weave_u(i, 0, on_scalar), lambda: weave_u(i, 1, on_vector if i % 2 else on_scalar)]
+            cut = 1 if i % 2 else 2
+            return (due, pieces[:cut], pieces[cut:], lambda: quantize(u_q[i], held["u", i][:]))
+
+        def lin_w2_job(jt):
+            pieces = [lambda: weave_lin_w2(jt, 0, on_scalar), lambda: weave_lin_w2(jt, 1, on_scalar)]
+            return (DEEP_STEP + jt, pieces, [], lambda: quantize(lin_w2_q[jt], held["lin_w2", jt][:]))
+
+        jobs = [u_job(1), w_job(4), w_job(6), u_job(2), u_job(3)] + [w_job(strip) for strip in (1, 3, 5, 7)]
+        jobs = jobs + [lin_w2_job(jt) for jt in range(4)]
+        scalar_side = {s: [] for s in range(len(UNITS))}
+        vector_first = {s: [] for s in range(len(UNITS))}
+        vector_side = {s: [] for s in range(len(UNITS))}
+        vector_side[HIDDEN_STEP].append(lambda: quantize(u_q[0], held["u", 0][:]))
+        count = 0
+        for due, pieces, own, finish in jobs:
+            for piece in pieces:
+                step = 2 + 2 * (count // 3) + (count % 3) // 2
+                scalar_side[step].append(piece)
+                count = count + 1
+            vector_first[min(due, step + 2)].extend(own)
+            vector_side[min(due, step + 2)].append(finish)
+        for gh in range(2):
+            step = min(DEEP_STEP, HIDDEN_STEP + 4 * gh + 3 + 2)
+            vector_first[step].append(lambda gh=gh: relu(gh))
+            vector_side[step].append(lambda gh=gh: quantize(hidden_q[gh], held["hidden", gh][:]))
+
+        def finish_x():
+            quantize(xx_q[0], held["xx0"][:])
+            xx1 = take(woven, "woven")
+            nc.vector.tensor_tensor(out=xx1[:], in0=held["x1"][:], in1=held["x1"][:], op=ALU.mult)
+            quantize(x_q[1], held["x1"][:])
+            quantize(xx_q[1], xx1[:])
+
+        vector_side[2].append(finish_x)
+        scalar_side[2].append(turn_vectors)
+
+        for s in range(2, len(UNITS)):
+            hidden_tile = s - HIDDEN_STEP
+            deep_tile = s - DEEP_STEP
             if s >= 3:
-                total_square(s - 3)
-            e_square(s - 1)
-            for job in early[s]:
+                square_total(s - 3)
+            square_e(s - 1)
+            if s == 3:
+                vectors_out()
+            for job in vector_first[s] + vector_side[s]:
                 job()
-            if s >= 2:
-                e_quant(s - 2)
-            e_round(s - 1, "G")
+            if 0 <= hidden_tile < 8:
+                hidden_matmuls(hidden_tile)
+            if deep_tile == 0:
+                first_and_deep(0)
+            quantize_e(s - 2)
+            round_e(s - 1)
             if s >= 4:
                 subtract(s - 4)
-            if s >= 2:
-                products(s - 2)
-            for job in mid[s]:
-                job()
+            whole_products(s - 2)
+            if s == LAST:
+                gather(2, (0, 1, 2))
             add_ids(s)
-            if s + 1 < len(UNITS):
+            if s < LAST:
                 embed(s + 1)
-            for job in late[s]:
+            if 0 <= hidden_tile < 8:
+                hidden_bias(hidden_tile)
+            if 1 <= deep_tile <= 3:
+                scale_with_deep(deep_tile - 1)
+                first_and_deep(deep_tile)
+            if s >= 4 and UNITS[s - 4][0] != WITH_DEEP[UNITS[s - 4][1]]:
+                if s < LAST:
+                    scale_on_gpsimd(s - 4)
+                else:
+                    scale_on_scalar(s - 4)
+            for job in scalar_side[s]:
                 job()
-        total_square(13)
-        e_square(15)
-        subtract(12)
-        e_quant(14)
-        products(14)
-        e_round(15, "V")
-        gather(2, (2, 3))
-        scale(12, "V")
-        subtract(13)
-        e_quant(15)
-        total_square(14)
-        last_products(0)
-        last_products(1)
-        scale(13, "G")
-        subtract(14)
-        last_square(0)
+            if deep_tile in (-2, -1):
+                gather(deep_tile + 2, (0, 1, 2))
+            if deep_tile in (1, 2):
+                gather(deep_tile - 1, (3,))
+            if deep_tile in (2, 3):
+                store(deep_tile - 2, sum_banks[deep_tile % 2], 0, M, on_scalar)
+
+        half_totals, half_squares = (e_banks[0], total_bank), (deep_bank, e_banks[1])
+        halves = [part(h, HALF) for h in range(2)]
+        square_total(LAST - 2)
+        square_e(LAST)
+        quantize_e(LAST - 1)
+        round_e(LAST)
+        subtract(LAST - 3)
+        whole_products(LAST - 1)
+        subtract(LAST - 2)
+        scale_with_deep(3)
+        square_total(LAST - 1)
+        scale_on_scalar(LAST - 2)
+        quantize_e(LAST)
+        for h in range(2):
+            products(LAST, half_totals[h], half_squares[h], HALF * h, HALF)
+        gather(2, (3,))
+        subtract(LAST - 1)
+        for h in range(2):
+            nc.scalar.activation(out=total_sq[LAST % 2][:, halves[h]], in_=half_totals[h][:, 0:HALF], func=ACT.Square)
+        scale_on_gpsimd(LAST - 1)
         gather(3, (0, 1))
-        scale(14, "V")
-        last_square(1)
-        finish(2, "S")
-        last_sub(0)
-        gather(3, (2,))
-        last_sub(1)
-        last_scale(0)
-        last_scale(1)
-        gather(3, (3,))
-        last_finish(0)
-        last_finish(1)
+        for h in range(2):
+            nc.vector.tensor_tensor(
+                out=term(LAST)[:, halves[h]], in0=total_sq[LAST % 2][:, halves[h]], in1=half_squares[h][:, 0:HALF], op=ALU.subtract
+            )
+        for h in range(2):
+            scale_on_scalar(LAST, halves[h])
+        store(2, sum_banks[0], 0, M, on_vector)
+        gather(3, (2, 3))
+        for h, copy in enumerate((on_scalar, on_vector)):
+            store(3, last_sum_banks[h], HALF * h, HALF, copy)

from contextlib import ExitStack

import concourse.mybir as mybir
from concourse.masks import make_identity

M, N, K, T, R, H = 512, 1024, 512, 512, 4, 1024
D = T * R
FLOPS = 2 * (N * K * D + 2 * M * N * D + M * N * T + M * N * H + M * H * T)

F32 = mybir.dt.float32
BF16 = mybir.dt.bfloat16
U32 = mybir.dt.uint32
U8 = mybir.dt.uint8
FP8X4 = mybir.dt.float8_e4m3fn_x4
ACT = mybir.ActivationFunctionType
ALU = mybir.AluOpType

P = 128
PASS = 512
STRIP = 256
HALF = M // 2

UNITS = [(r, jt) for r in range(R) for jt in (0, 1)] + [(r, jt) for jt in (2, 3) for r in range(R)]
LAST = len(UNITS) - 1

HIDDEN_STEP = 3
DEEP_STEP = HIDDEN_STEP + 8
WITH_DEEP = (3, 3, 2, 0)
WITH_B0 = 1


def strip_of(unit):
    r, jt = UNITS[unit]
    return 2 * r + jt // 2


def tile_attribute_fm_plus_mlp_f4_kernel(tc, x, attr, w_attr, ids, pair, lin, b0, u, b1, w2, out):
    nc = tc.nc
    with ExitStack() as ctx:
        sb = ctx.enter_context(tc.tile_pool(name="sb", bufs=1))
        ps = ctx.enter_context(tc.psum_pool(name="ps", bufs=1))
        ctx.enter_context(tc.manual_schedule())

        def tiles(name, count, width, dtype):
            return [sb.tile([P, width], dtype, name="%s%d" % (name, i), align_bytes=64) for i in range(count)]

        def mx_tiles(name, count, width):
            return list(zip(tiles(name + "_c", count, width, U32), tiles(name + "_s", count, width, U8)))

        banks = [ps.tile([P, PASS], F32, name="bank%d" % i) for i in range(8)]
        e_banks, total_bank, square_banks, deep_bank, sum_banks = banks[0:2], banks[2], banks[3:5], banks[5], banks[6:8]
        turn_banks = banks[2:8]

        attr_raw = tiles("attr_raw", 2, 4 * K, BF16)
        x_raw = tiles("x_raw", 2, 4 * PASS, BF16)
        w_raw = tiles("w_raw", D // STRIP, 4 * STRIP, BF16)
        ids_raw = tiles("ids_raw", 2 * D // STRIP, 4 * STRIP, BF16)
        u_raw = tiles("u_raw", 4, 4 * PASS, BF16)
        lin_w2_raw = tiles("lin_w2_raw", 2, 8 * T, BF16)
        vec_raw = tiles("vec_raw", 1, P, BF16)[0]
        vec_rows = tiles("vec_rows", 1, P, F32)[0]
        gains = tiles("gains", 1, D // P, F32)[0]
        b0_cols = tiles("b0_cols", 1, T // P, F32)[0]
        b1_slots = tiles("b1_slots", 1, 8, BF16)[0]
        ident = tiles("ident", 1, P, F32)[0]

        woven = tiles("woven", 10, 4 * PASS, BF16)
        attr_q = mx_tiles("attr", 2, PASS)
        x_q = mx_tiles("x", 2, M)
        xx_q = mx_tiles("xx", 2, M)
        w_q = mx_tiles("w", D // STRIP, STRIP)
        u_q = mx_tiles("u", 4, PASS)
        hidden_q = mx_tiles("hidden", 2, M)
        lin_w2_q = mx_tiles("lin_w2", 4, 4 * P)
        e_q = mx_tiles("e", 2, 2 * P)
        ee_q = mx_tiles("ee", 2, 2 * P)
        e32 = tiles("e32", 2, 8 * P, F32)
        e_bf = tiles("e_bf", 1, 8 * P, BF16)[0]
        ee_bf = tiles("ee_bf", 2, 8 * P, BF16)
        total_sq = tiles("total_sq", 2, M, F32)
        terms = tiles("terms", 8, M, F32)
        result = tiles("result", 2, M, F32)
        taken = {"woven": 0, "turn": 0}
        held = {}

        def take(ring, name):
            taken[name] = taken[name] + 1
            return ring[(taken[name] - 1) % len(ring)]

        def on_scalar(dst, src):
            nc.scalar.copy(out=dst, in_=src)

        def on_vector(dst, src):
            nc.vector.tensor_copy(out=dst, in_=src)

        def quantize(q, src):
            nc.vector.quantize_mx(out=q[0][:].bitcast(FP8X4), scales=q[1][:], in_=src)

        def mx(dst, lhs, lhs_col, rhs, rhs_col, n, start, stop):
            nc.tensor.matmul_mx(
                out=dst,
                lhsT=lhs[0][:, lhs_col : lhs_col + P].bitcast(FP8X4),
                lhsT_scale=lhs[1][:, lhs_col : lhs_col + P],
                rhs=rhs[0][:, rhs_col : rhs_col + n].bitcast(FP8X4),
                rhs_scale=rhs[1][:, rhs_col : rhs_col + n],
                start=start,
                stop=stop,
            )

        def part(i, width):
            return slice(width * i, width * (i + 1))

        def slots(tile):
            return tile[:].rearrange("p (t c) -> p t c", t=4)

        def walk_woven(ap):
            return ap.rearrange("p (c i t) -> p c t i", i=4, t=4)

        def walk_slots(ap):
            return ap.rearrange("p t (c i) -> p c t i", i=4)

        def load_rows(dst, src):
            nc.sync.dma_start(out=slots(dst), in_=src.rearrange("(p t) c -> p t c", t=4))

        def load_x(g):
            nc.sync.dma_start(
                out=x_raw[g][:].rearrange("p (s c) -> p s c", s=4),
                in_=x[:, part(g, PASS)].rearrange("(s p) c -> p s c", p=P),
            )

        def load_w(strip):
            load_rows(w_raw[strip], w_attr[:, part(strip, STRIP)])

        def load_ids(strip):
            for g in range(2):
                load_rows(ids_raw[2 * strip + g], ids[part(g, PASS), part(strip, STRIP)])

        def load_u(gh):
            for g in range(2):
                load_rows(u_raw[2 * gh + g], u[part(g, PASS), part(gh, PASS)])

        load_rows(attr_raw[0], attr[part(0, PASS), :])
        load_rows(attr_raw[1], attr[part(1, PASS), :])
        load_w(0)
        load_x(0)
        load_ids(0)
        load_w(2)
        load_x(1)
        load_u(0)
        load_ids(2)
        load_w(4)
        load_w(6)
        nc.sync.dma_start(out=vec_raw[0:16, :], in_=pair.rearrange("(i c) -> i c", c=P))
        nc.sync.dma_start(out=vec_raw[16:20, :], in_=b0.rearrange("(i c) -> i c", c=P))
        nc.sync.dma_start(
            out=b1_slots[:].rearrange("p (g t) -> p g t", g=2), in_=b1.rearrange("(g p t) -> p g t", g=2, t=4)
        )
        load_u(1)
        load_ids(4)
        load_ids(6)
        for strip in (1, 3, 5, 7):
            load_w(strip)
        load_ids(1)
        load_ids(3)
        for raw, src in zip(lin_w2_raw, (lin, w2)):
            nc.sync.dma_start(
                out=raw[:].rearrange("p (g c) -> p g c", g=2), in_=src.rearrange("(g p t) c -> p g (t c)", g=2, t=4)
            )
        load_ids(5)
        load_ids(7)

        def turn(raw, b, key):
            words = raw[:].bitcast(F32)
            bank = take(turn_banks, "turn")
            for s in range(2):
                for w in range(2):
                    first = 256 * (2 * b + s)
                    nc.tensor.transpose(bank[:, part(2 * s + w, P)], words[:, first + w : first + 256 : 2], ident[:])
            if b == 0:
                held[key] = take(woven, "woven")
            held[key, b] = bank

        def turn_out(key, b, copy):
            copy(
                held[key][:].bitcast(F32)[:, part(b, PASS)].rearrange("p (s m w) -> p s m w", s=2, w=2),
                held[key, b][:].rearrange("p (s w m) -> p s m w", s=2, w=2),
            )

        def turn_both(raw, key, copies):
            for b in range(2):
                turn(raw, b, key)
                turn_out(key, b, copies[b])

        def weave_w(strip, copy):
            held["w", strip] = take(woven, "woven")
            copy(walk_woven(held["w", strip][:, 0 : 4 * STRIP]), walk_slots(slots(w_raw[strip])))

        def quantize_w(strip):
            quantize(w_q[strip], held["w", strip][:, 0 : 4 * STRIP])

        def weave_u(i, piece, copy):
            if piece == 0:
                held["u", i] = take(woven, "woven")
            copy(
                held["u", i][:].rearrange("p (v m t) -> p m t v", v=4, t=4)[:, part(piece, 64)],
                u_raw[i][:].rearrange("p (t m v) -> p m t v", t=4, v=4)[:, part(piece, 64)],
            )

        def weave_lin_w2(jt, piece, copy):
            if piece == 0:
                held["lin_w2", jt] = take(woven, "woven")
            src = lin_w2_raw[piece][:].rearrange("p (g t c) -> p g t c", g=2, t=4)[:, :, :, part(jt, P)]
            copy(
                held["lin_w2", jt][:, part(piece, 8 * P)].rearrange("p (g c i t) -> p g c t i", g=2, i=4, t=4),
                src.rearrange("p g t (c i) -> p g c t i", i=4),
            )

        def turn_vectors():
            nc.scalar.copy(out=vec_rows[0:20, :], in_=vec_raw[0:20, :])
            nc.tensor.transpose(sum_banks[0][:, 0:P], vec_rows[:], ident[:])

        def vectors_out():
            nc.scalar.activation(out=gains[:], in_=sum_banks[0][:, 0:16], func=ACT.Copy, scale=0.5)
            nc.scalar.copy(out=b0_cols[:], in_=sum_banks[0][:, 16:20])

        def hidden_matmuls(i):
            gh, s = divmod(i, 4)
            for v in range(4):
                for g in range(2):
                    mx(deep_bank[:, part(v, P)], u_q[2 * gh + g], P * v, x_q[g], P * s, P, g == 0, g == 1)

        def hidden_bias(i):
            gh, s = divmod(i, 4)
            if s == 0:
                held["hidden", gh] = take(woven, "woven")
            nc.vector.tensor_tensor(
                out=held["hidden", gh][:, part(s, PASS)].rearrange("p (m v) -> p m v", v=4),
                in0=deep_bank[:].rearrange("p (v m) -> p m v", v=4),
                in1=b1_slots[:, part(gh, 4)].unsqueeze(1).to_broadcast([P, P, 4]),
                op=ALU.add,
            )

        def relu(gh):
            tile = held["hidden", gh]
            nc.vector.tensor_scalar(out=tile[:], in0=tile[:], scalar1=0.0, scalar2=None, op0=ALU.max)

        def first_and_deep(jt):
            for i, rhs in enumerate(x_q + hidden_q):
                mx(deep_bank[:], lin_w2_q[jt], P * i, rhs, 0, M, i == 0, i == 3)

        def embed(n, passes=(0, 1)):
            for g in passes:
                for t in range(4):
                    mx(e_banks[g][:, part(t, P)], attr_q[g], P * t, w_q[strip_of(n)], P * (UNITS[n][1] % 2), P, True, True)

        def add_ids(n, passes=(0, 1)):
            for g in passes:
                nc.vector.tensor_tensor(
                    out=e32[n % 2][:].rearrange("p (t g c) -> p t g c", t=4, g=2)[:, :, g, :],
                    in0=slots(e_banks[g]),
                    in1=slots(ids_raw[2 * strip_of(n) + g])[:, :, part(UNITS[n][1] % 2, P)],
                    op=ALU.add,
                )

        def round_e(n):
            nc.gpsimd.tensor_scalar(
                out=walk_woven(e_bf[:]), in0=walk_slots(slots(e32[n % 2])), scalar1=1.0, scalar2=0.0, op0=ALU.mult, op1=ALU.add
            )

        def square_e(n):
            nc.scalar.activation(out=walk_woven(ee_bf[n % 2][:]), in_=walk_slots(slots(e32[n % 2])), func=ACT.Square)

        def quantize_e(n):
            quantize(e_q[n % 2], e_bf[:])
            quantize(ee_q[n % 2], ee_bf[n % 2][:])

        def products(n, to_total, to_squares, first_sample, samples):
            for g in range(2):
                mx(to_total[:, 0:samples], e_q[n % 2], P * g, x_q[g], first_sample, samples, g == 0, g == 1)
            for g in range(2):
                mx(to_squares[:, 0:samples], ee_q[n % 2], P * g, xx_q[g], first_sample, samples, g == 0, g == 1)

        def whole_products(n):
            products(n, total_bank, square_banks[n % 2], 0, M)

        def square_total(n):
            nc.scalar.activation(out=total_sq[n % 2][:], in_=total_bank[:], func=ACT.Square)

        def term(n):
            return terms[n % len(terms)]

        def subtract(n):
            nc.vector.tensor_tensor(out=term(n)[:], in0=total_sq[n % 2][:], in1=square_banks[n % 2][:], op=ALU.subtract)

        def gain(n):
            r, jt = UNITS[n]
            return gains[:, part(4 * r + jt, 1)]

        def scale_on_gpsimd(n):
            r, jt = UNITS[n]
            shift = b0_cols[:, part(jt, 1)] if r == WITH_B0 else 0.0
            nc.gpsimd.tensor_scalar(out=term(n)[:], in0=term(n)[:], scalar1=gain(n), scalar2=shift, op0=ALU.mult, op1=ALU.add)

        def scale_on_scalar(n, cols=slice(0, M)):
            r, jt = UNITS[n]
            shift = b0_cols[:, part(jt, 1)] if r == WITH_B0 else 0.0
            nc.scalar.activation(out=term(n)[:, cols], in_=term(n)[:, cols], func=ACT.Identity, scale=gain(n), bias=shift)

        def scale_with_deep(jt):
            n = UNITS.index((WITH_DEEP[jt], jt))
            nc.vector.scalar_tensor_tensor(
                out=term(n)[:], in0=term(n)[:], scalar=gain(n), in1=deep_bank[:], op0=ALU.mult, op1=ALU.add
            )

        last_sum_banks = (sum_banks[1], square_banks[0])

        def gather(jt, components):
            width = 2 if jt == 3 else 4
            for r in components:
                for s in range(4):
                    bank = last_sum_banks[s // 2] if jt == 3 else sum_banks[jt % 2]
                    nc.tensor.matmul(
                        out=bank[:, part(s % width, P)],
                        lhsT=term(UNITS.index((r, jt)))[:, part(s, P)],
                        rhs=ident[:],
                        start=(r == 0 and s % width == 0),
                        stop=(r == R - 1 and s % width == width - 1),
                        is_transpose=True,
                    )

        def store(jt, bank, first_sample, samples, copy):
            staged = result[jt % 2][:, first_sample : first_sample + samples]
            copy(staged, bank[:, 0:samples])
            nc.sync.dma_start(
                out=out[first_sample : first_sample + samples, part(jt, P)].rearrange("(s p) c -> p s c", p=P),
                in_=staged.rearrange("p (s c) -> p s c", c=P),
            )

        make_identity(nc, ident[:])
        nc.scalar.activation(out=vec_rows[:], in_=ident[:], func=ACT.Square, scale=0.0)
        turn_both(attr_raw[0], "attr0", (on_scalar, on_vector))
        turn_both(attr_raw[1], "attr1", (on_scalar, on_scalar))
        weave_w(strip_of(0), on_vector)
        quantize(attr_q[0], held["attr0"][:])
        turn_both(x_raw[0], "x0", (on_scalar, on_scalar))
        quantize_w(strip_of(0))
        quantize(attr_q[1], held["attr1"][:])
        embed(0)
        add_ids(0, (0,))
        embed(1, (0,))
        quantize(x_q[0], held["x0"][:])
        held["xx0"] = take(woven, "woven")
        nc.scalar.activation(out=held["xx0"][:], in_=held["x0"][:], func=ACT.Square)
        weave_w(strip_of(2), on_vector)
        turn(x_raw[1], 0, "x1")
        turn_out("x1", 0, on_scalar)
        turn(x_raw[1], 1, "x1")
        quantize_w(strip_of(2))
        add_ids(0, (1,))
        embed(1, (1,))
        weave_u(0, 0, on_scalar)
        square_e(0)
        round_e(0)
        add_ids(1, (0,))
        turn_out("x1", 1, on_vector)
        add_ids(1, (1,))
        embed(2)
        weave_u(0, 1, on_scalar)

        def w_job(strip):
            due = [strip_of(n) for n in range(len(UNITS))].index(strip) - 1
            return (due, [lambda: weave_w(strip, on_scalar)], [], lambda: quantize_w(strip))

        def u_job(i):
            due = HIDDEN_STEP + 4 * (i // 2)
            pieces = [lambda: weave_u(i, 0, on_scalar), lambda: weave_u(i, 1, on_vector if i % 2 else on_scalar)]
            cut = 1 if i % 2 else 2
            return (due, pieces[:cut], pieces[cut:], lambda: quantize(u_q[i], held["u", i][:]))

        def lin_w2_job(jt):
            pieces = [lambda: weave_lin_w2(jt, 0, on_scalar), lambda: weave_lin_w2(jt, 1, on_scalar)]
            return (DEEP_STEP + jt, pieces, [], lambda: quantize(lin_w2_q[jt], held["lin_w2", jt][:]))

        jobs = [u_job(1), w_job(4), w_job(6), u_job(2), u_job(3)] + [w_job(strip) for strip in (1, 3, 5, 7)]
        jobs = jobs + [lin_w2_job(jt) for jt in range(4)]
        scalar_side = {s: [] for s in range(len(UNITS))}
        vector_first = {s: [] for s in range(len(UNITS))}
        vector_side = {s: [] for s in range(len(UNITS))}
        vector_side[HIDDEN_STEP].append(lambda: quantize(u_q[0], held["u", 0][:]))
        count = 0
        for due, pieces, own, finish in jobs:
            for piece in pieces:
                step = 2 + 2 * (count // 3) + (count % 3) // 2
                scalar_side[step].append(piece)
                count = count + 1
            vector_first[min(due, step + 2)].extend(own)
            vector_side[min(due, step + 2)].append(finish)
        for gh in range(2):
            step = min(DEEP_STEP, HIDDEN_STEP + 4 * gh + 3 + 2)
            vector_first[step].append(lambda gh=gh: relu(gh))
            vector_side[step].append(lambda gh=gh: quantize(hidden_q[gh], held["hidden", gh][:]))

        def finish_x():
            quantize(xx_q[0], held["xx0"][:])
            xx1 = take(woven, "woven")
            nc.vector.tensor_tensor(out=xx1[:], in0=held["x1"][:], in1=held["x1"][:], op=ALU.mult)
            quantize(x_q[1], held["x1"][:])
            quantize(xx_q[1], xx1[:])

        vector_side[2].append(finish_x)
        scalar_side[2].append(turn_vectors)

        for s in range(2, len(UNITS)):
            hidden_tile = s - HIDDEN_STEP
            deep_tile = s - DEEP_STEP
            if s >= 3:
                square_total(s - 3)
            square_e(s - 1)
            if s == 3:
                vectors_out()
            for job in vector_first[s] + vector_side[s]:
                job()
            if 0 <= hidden_tile < 8:
                hidden_matmuls(hidden_tile)
            if deep_tile == 0:
                first_and_deep(0)
            quantize_e(s - 2)
            round_e(s - 1)
            if s >= 4:
                subtract(s - 4)
            whole_products(s - 2)
            if s == LAST:
                gather(2, (0, 1, 2))
            add_ids(s)
            if s < LAST:
                embed(s + 1)
            if 0 <= hidden_tile < 8:
                hidden_bias(hidden_tile)
            if 1 <= deep_tile <= 3:
                scale_with_deep(deep_tile - 1)
                first_and_deep(deep_tile)
            if s >= 4 and UNITS[s - 4][0] != WITH_DEEP[UNITS[s - 4][1]]:
                if s < LAST:
                    scale_on_gpsimd(s - 4)
                else:
                    scale_on_scalar(s - 4)
            for job in scalar_side[s]:
                job()
            if deep_tile in (-2, -1):
                gather(deep_tile + 2, (0, 1, 2))
            if deep_tile in (1, 2):
                gather(deep_tile - 1, (3,))
            if deep_tile in (2, 3):
                store(deep_tile - 2, sum_banks[deep_tile % 2], 0, M, on_scalar)

        half_totals, half_squares = (e_banks[0], total_bank), (deep_bank, e_banks[1])
        halves = [part(h, HALF) for h in range(2)]
        square_total(LAST - 2)
        square_e(LAST)
        quantize_e(LAST - 1)
        round_e(LAST)
        subtract(LAST - 3)
        whole_products(LAST - 1)
        subtract(LAST - 2)
        scale_with_deep(3)
        square_total(LAST - 1)
        scale_on_scalar(LAST - 2)
        quantize_e(LAST)
        for h in range(2):
            products(LAST, half_totals[h], half_squares[h], HALF * h, HALF)
        gather(2, (3,))
        subtract(LAST - 1)
        for h in range(2):
            nc.scalar.activation(out=total_sq[LAST % 2][:, halves[h]], in_=half_totals[h][:, 0:HALF], func=ACT.Square)
        scale_on_gpsimd(LAST - 1)
        gather(3, (0, 1))
        for h in range(2):
            nc.vector.tensor_tensor(
                out=term(LAST)[:, halves[h]], in0=total_sq[LAST % 2][:, halves[h]], in1=half_squares[h][:, 0:HALF], op=ALU.subtract
            )
        for h in range(2):
            scale_on_scalar(LAST, halves[h])
        store(2, sum_banks[0], 0, M, on_vector)
        gather(3, (2, 3))
        for h, copy in enumerate((on_scalar, on_vector)):
            store(3, last_sum_banks[h], HALF * h, HALF, copy)
